import numpy as np, ml_dtypes
CORES = [10,34,74,98]
N = 4
import mx_ref
BF = ml_dtypes.bfloat16
def pick(q, e):
    c = np.concatenate([q[0].reshape(128, -1, 4), np.zeros((128, 1, 4), np.uint8)], axis=1); s = np.concatenate([q[1], np.ones((16, 1), np.uint8)], axis=1)
    return (np.ascontiguousarray(c[:, e].reshape(128, -1)), np.ascontiguousarray(s[:, e]))
def join(*qs):
    return (np.concatenate([q[0] for q in qs], axis=1), np.concatenate([q[1] for q in qs], axis=1))
def put(q, e, v):
    c, s = q[0].reshape(128, -1, 4).copy(), q[1].copy(); c[:, e] = v[0].reshape(128, -1, 4); s[:, e] = v[1]
    return (c.reshape(128, -1), s)
def pk(c, s):
    return (np.ascontiguousarray(c), mx_ref.live(s))
def emit(q):
    return q[0], q[1]
def cols(t, e):
    v = np.concatenate([t.reshape(128, -1, 4), np.zeros((128, 1, 4), BF)], axis=1)
    return np.ascontiguousarray(v[:, e]).reshape(128, -1)
def tile(rs):
    return np.stack(rs, axis=2).reshape(128, -1).astype(BF)
def cut(t, i, w=512):
    return t[:, w * i:w * i + w]
def f(rng, *shape):
    return mx_ref.flush((rng.standard_normal(shape, dtype=np.float32) * np.exp2(rng.integers(-2, 3, shape[:-1] + (1,)))).astype(BF))
def wide(rng, *shape, cols=0):
    v = rng.standard_normal(shape, dtype=np.float32) * np.exp2(rng.integers(-12, 13, shape)).astype(np.float32)
    if cols: v *= np.repeat(np.exp2(rng.integers(-cols, cols + 1, shape[:-2] + (1, shape[-1] // 4))) * (rng.random(shape[:-2] + (1, shape[-1] // 4)) > 0.0625), 4, axis=-1).astype(np.float32)
    return mx_ref.flush(v.astype(BF))
P, K, O = 256, 64, 1
E = P + 2 * K // N
def play(x, u, a, b):
    row = mx_ref.quantize(np.concatenate([x[r] for r in range(N)], axis=1))
    num = 4 * np.arange(N * P)
    k = mx_ref.quantize(np.ascontiguousarray(u[0]))
    high = []
    for t in range(2):
        n = num.size
        s = mx_ref.matmul(k, row)[0] + np.float32(0)
        split = np.sort(np.argsort(-s, kind="stable")[:K])
        parents = pick(row, split)
        kids = []
        for m in (a[0], b[0]):
            kids.append(tile([mx_ref.matmul(mx_ref.quantize(np.ascontiguousarray(cut(m, i))), parents) * np.float32(0.0625) for i in range(4)]))
        size = np.max(np.abs(np.stack(kids).astype(np.float32)).reshape(2, 16, 8, K, 4), axis=(2, 4))
        high.append((np.max(np.abs(s)), np.max(size), np.min(np.where(size == 0, np.float32(1), size))))
        e = np.repeat(np.arange(n), 1 + np.isin(np.arange(n), split))
        first = split + np.arange(K)
        num = num[e]
        num[first + 1] += 2 - t
        e[first] = n + np.arange(K)
        e[first + 1] = n + K + np.arange(K)
        row = pick(join(row, mx_ref.quantize(kids[0]), mx_ref.quantize(kids[1])), e)
    return row, num, high
def times(t, v):
    return mx_ref.flush((t.astype(np.float32) * np.float32(v)).astype(BF))
def lift(d, r, e, v):
    s = np.where(d["u"][0][:, None, :4].astype(np.float32) < 0, -v, v)
    x = np.array(d["x"][r].astype(np.float32)).reshape(128, P, 4)
    x[:, e] = np.abs(x[:, e]) * s
    d["x"][r] = mx_ref.flush(x.reshape(128, -1).astype(BF))
def setup_inputs(rng):
    u = np.array(f(rng, 128, 512))
    u[:, 4:] = 0
    return {"x": np.array(f(rng, N, 128, 4 * P)), "u": np.stack([u] * N), "a": np.stack([f(rng, 128, 2048)] * N), "b": np.stack([f(rng, 128, 2048)] * N), "w": f(rng, N, 128, 512 * O)}
def setup_inputs_below(rng):
    d = setup_inputs(rng)
    d["x"] = np.array(times(d["x"], 2.0 ** 20))
    for r in range(N): lift(d, r, np.arange(P), -1)
    lift(d, N - 1, rng.permutation(P)[:K], -2.0 ** -6)
    v, p = d["a"][0].astype(np.float32) * np.float32(2.0 ** -6), np.arange(128)
    for i in range(4): v[p, 512 * i + 4 * p + i] = 128
    d["a"] = np.stack([mx_ref.flush(v.astype(BF))] * N)
    d["b"] = times(d["a"], 2.0 ** -4)
    return d
def setup_inputs_edge(rng):
    d = setup_inputs(rng)
    d["a"], d["b"], d["x"] = times(d["a"], 2.0 ** -12), times(d["b"], 2.0 ** -12), np.array(times(d["x"], 64))
    lift(d, int(rng.integers(1, N - 1)), rng.permutation(P)[:K], 4096)
    lift(d, N - 1, rng.permutation(P)[:K], 64)
    return d
def setup_inputs_spread(rng):
    return {**setup_inputs(rng), "x": wide(rng, N, 128, 4 * P, cols=6)}
def setup_inputs_ties(rng):
    d = setup_inputs(rng)
    v, e = times(f(rng, 128, 24), 2.0 ** 14), (rng.permutation(N * P) % 6).reshape(N, P)
    d["x"] = np.stack([cols(v, e[r]) for r in range(N)])
    lift(d, N - 1, rng.permutation(P)[:K // 8], 64)
    return {**d, "b": d["a"].copy()}
def setup_inputs_zero(rng):
    d = setup_inputs(rng)
    d["u"][:, 64:] = 0
    for r in range(N):
        kind = rng.permutation(P) % 3
        lift(d, r, np.flatnonzero(kind == 2), -1)
        x = np.array(d["x"][r]).reshape(128, P, 4)
        x[:, kind == 0] = 0
        x[:64, kind == 1] = 0
        d["x"][r] = x.reshape(128, -1)
    return d
def check_inputs(d):
    b = []
    for k in ("x", "u", "a", "b", "w"):
        v = np.abs(d[k].astype(np.float32))
        if not (np.isfinite(v).all() and ((v == 0) | (v >= 2.0 ** -30) & (v <= 2.0 ** 30)).all()): b.append("a value of " + k)
    if (d["u"][:, :, 4:].astype(np.float32) != 0).any(): b.append("u has numbers behind its column 0")
    for k in ("u", "a", "b"):
        v = d[k].astype(np.float32)
        if (v != v[:1]).any(): b.append(k + " differs between ranks")
    if not b:
        try:
            high = play(d["x"], d["u"], d["a"], d["b"])[2]
            if not all(np.isfinite(s) for s, c, m in high): b.append("a score")
            if not all(c <= 2.0 ** 30 and m >= 2.0 ** -30 for s, c, m in high): b.append("a number of a child")
        except Exception:
            b.append("a number of a child")
    return b
def reference(x, u, a, b, w):
    row, num, _ = play(x, u, a, b)
    oc, osc = np.zeros((N, 128, 4 * E), np.uint8), np.zeros((N, 16, E), np.uint8)
    hs, y = np.zeros((N, 1, E), np.float32), np.zeros((N, 128, O * E), np.float32)
    for r in range(N):
        q = pick(row, np.arange(r * E, r * E + E))
        oc[r], osc[r] = emit(q)
        hs[r, 0] = num[r * E:r * E + E]
        for o in range(O):
            y[r, :, o * E:o * E + E] = mx_ref.matmul(mx_ref.quantize(np.ascontiguousarray(cut(w[r], o))), q)
    return {"oc": oc, "osc": osc, "hs": hs, "y": y}

@@ -1,0 +1,475 @@
+from concourse.bass import DstId, RemoteDMATransfer
+from concourse.mybir import dt, AluOpType as Alu, AxisListType, ActivationFunctionType as Act
+
+N, P, K, E = 4, 256, 64, 288
+LEN = (1024, 1088)
+CH = ([(128 * c, 0, 4, c // 2) for c in range(8)],
+      [(0, 0, 4, 0), (128, 0, 4, 0), (256, 0, 4, 1), (384, 0, 4, 1), (512, 0, 4, 2), (640, 0, 4, 2), (736, 1, 3, 2), (832, 0, 4, 3), (960, 0, 4, 3)])
+WIN = ([(0, 288), (160, 576), (448, 864), (736, 1024)], [(0, 288), (224, 576), (512, 864), (800, 1088)], [(E * r, E * r + E) for r in range(N)])
+NEED = ([(0, 288), (0, 576), (448, 1024), (736, 1024)], [(0, 288), (0, 576), (512, 1088), (800, 1088)])
+F32, BF, I32, U16 = "float32", "bfloat16", "int32", "uint16"
+CW = 131
+
+SCRATCH = {
+    "xt": ("sbuf", [128, 1024], BF), "uin": ("sbuf", [128, 8], BF), "ut": ("sbuf", [128, 512], BF), "uz": ("sbuf", [128, 128], BF),
+    "at": ("sbuf", [128, 2048], BF), "bt": ("sbuf", [128, 2048], BF), "wt": ("sbuf", [128, 512], BF),
+    "sp": ("sbuf", [128, 1024], F32), "rep": ("sbuf", [128, 1024], F32), "carry": ("sbuf", [128, 1024], F32),
+    "msp": ("sbuf", [128, 640], BF), "mrep": ("sbuf", [128, 640], BF), "ones": ("sbuf", [128, 640], BF), "carb": ("sbuf", [128, 640], BF),
+    "pi": ("sbuf", [128, 4], I32), "dcol": ("sbuf", [128, 2], F32),
+    "psc": ("psum", [128, 2048], F32), "pch": ("psum", [128, 2048], F32),
+    "ysb": ("sbuf", [128, 288], F32), "hsr": ("sbuf", [128, 288], F32),
+    "tn0": ("sbuf", [128, 1248], F32), "tn1": ("sbuf", [128, 1056], F32),
+}
+for _q, _n in (("u", 128), ("a", 512), ("b", 512), ("w", 128), ("r0", 1248), ("r1", 1056), ("r2", 288)):
+    SCRATCH[_q + "c"] = ("sbuf", [128, _n], "float8_e4m3fn_x4")
+    SCRATCH[_q + "s"] = ("sbuf", [128, _n], "uint8")
+for _t in range(2):
+    for _n, _w, _d in (("ha", 1664, BF), ("hb", 1664, BF), ("row", 1088, F32), ("own", 4, F32), ("land", 8, F32), ("cmp", 5 * 1216, BF),
+                       ("eq", 640, BF), ("sg", 2 * 1088, BF), ("sj", 2 * 1088, BF), ("so", 5 * 608, BF), ("neg", 2, F32), ("acc", 4, F32), ("tri", 2, F32),
+                       ("rho", 2, F32), ("mk", 5, F32), ("mrow", 640, BF), ("fb", 644, F32), ("ca", 6 * CW, F32), ("cp", 6 * CW, F32), ("cum", 6 * CW + 4, F32),
+                       ("jt", 30, F32), ("jj", 30, F32), ("fs", 12 * CW, BF), ("sa", 6, F32), ("sb", 6, F32), ("xa", 6, F32), ("xb", 6, F32),
+                       ("dd", 6, F32), ("ll", 6, F32), ("wf", 24, F32), ("wu", 24, U16)):
+        SCRATCH["%s%d" % (_n, _t)] = ("sbuf", [128, _w], _d)
+SEMAPHORES = ["v", "s", "p", "gc", "sent", "arr0", "arr1", "arrw", "dx", "du", "da", "db", "dw", "out"]
+
+
+def rank_program(g, core, T, topo):
+    r = T.rank_of(core)
+    if r is None:
+        return
+    Q = {"v": g.vector, "s": g.scalar, "p": g.tensor, "g": g, "y": g.sync}
+    ESEM = {"v": "v", "s": "s", "p": "p", "g": "gc"}
+    total, known, hist = {}, {q: {} for q in Q}, {}
+
+    def V(name, c0=0, c1=None, step=1, p0=0, p1=128):
+        if c1 is None:
+            c1 = SCRATCH[name][1][1]
+        ap = T[name][p0:p1, c0:c1] if step == 1 else T[name][p0:p1, c0:c1:step]
+        return (ap, name, c0, c1, step, p0, p1)
+
+    def clash(x, y):
+        if SCRATCH[x[1]][0] == "psum":
+            return x[2] // 512 <= (y[3] - 1) // 512 and y[2] // 512 <= (x[3] - 1) // 512
+        if x[6] <= y[5] or y[6] <= x[5] or x[3] <= y[2] or y[3] <= x[2]:
+            return False
+        return not (x[4] == y[4] and x[4] > 1 and (x[2] - y[2]) % x[4] != 0)
+
+    def need(q, reads, writes):
+        todo = {}
+        for acc, wr in [(a, False) for a in reads] + [(a, True) for a in writes]:
+            psum = SCRATCH[acc[1]][0] == "psum"
+            for old, owr, s, n, clock, oq in hist.get(acc[1], []):
+                if not (wr or owr or (psum and oq != q)) or known[q].get(s, 0) >= n or not clash(acc, old):
+                    continue
+                if s not in todo or todo[s][0] < n:
+                    todo[s] = (n, clock)
+        for s in sorted(todo):
+            n, clock = todo[s]
+            if known[q].get(s, 0) < n:
+                Q[q].wait_ge(T.sem[s], n)
+                known[q][s] = n
+                for s2, n2 in clock.items():
+                    known[q][s2] = max(known[q].get(s2, 0), n2)
+
+    def note(q, reads, writes, s, n):
+        clock = dict(known[q])
+        for acc, wr in [(a, False) for a in reads] + [(a, True) for a in writes]:
+            hist.setdefault(acc[1], []).append((acc, wr, s, n, clock, q))
+
+    def op(q, call, reads, writes):
+        need(q, reads, writes)
+        s = ESEM[q]
+        total[s] = total.get(s, 0) + 1
+        call().then_inc(T.sem[s], 1)
+        note(q, reads, writes, s, total[s])
+
+    def dma(q, out, in_, sem, reads, writes):
+        need(q, reads, writes)
+        total[sem] = total.get(sem, 0) + 16
+        Q[q].dma_start(out, in_).then_inc(T.sem[sem], 16)
+        note(q, reads, writes, sem, total[sem])
+
+    def sc(x):
+        return x[0] if isinstance(x, tuple) else x
+
+    def ts(out, in0, s1, s2, op0, op1=None):
+        rd = [x for x in (in0, s1, s2) if isinstance(x, tuple)]
+        if op1 is None:
+            op("v", lambda: g.vector.tensor_scalar(out[0], in0[0], sc(s1), None, op0), rd, [out])
+        else:
+            op("v", lambda: g.vector.tensor_scalar(out[0], in0[0], sc(s1), sc(s2), op0, op1), rd, [out])
+
+    def tt(out, a, b, o):
+        op("v", lambda: g.vector.tensor_tensor(out[0], a[0], b[0], o), [a, b], [out])
+
+    def copy(q, out, in_):
+        if q == "v":
+            op("v", lambda: g.vector.tensor_copy(out[0], in_[0]), [in_], [out])
+        else:
+            op("s", lambda: g.scalar.activation(out[0], in_[0], Act.Copy), [in_], [out])
+
+    def act(out, in_, f, bias=0.0, scale=1.0, accum=None):
+        rd = [in_] + [x for x in (bias, scale) if isinstance(x, tuple)]
+        if accum is None:
+            op("s", lambda: g.scalar.activation(out[0], in_[0], f, bias=sc(bias), scale=sc(scale)), rd, [out])
+        else:
+            op("s", lambda: g.scalar.activation(out[0], in_[0], f, bias=sc(bias), scale=sc(scale), accum_out=accum[0]), rd, [out, accum])
+
+    def scan(out, a, b, initial, o0, o1):
+        op("v", lambda: g.vector.tensor_tensor_scan(out[0], a[0], b[0], initial, o0, o1), [a, b], [out])
+
+    def turn(out, in_):
+        op("v", lambda: g.vector.transpose(out[0], in_[0]), [in_], [out])
+
+    def fill(out, c):
+        op("v", lambda: g.vector.memset(out[0], c), [], [out])
+
+    def quant(q, a, b, in_):
+        c, s = V(q + "c", a, b), V(q + "s", a, b)
+        op("v", lambda: g.vector.quantize_mx(c[0], s[0], in_[0]), [in_], [c, s])
+
+    def mm(bank, q1, a1, q2, a2, n):
+        o = V(bank[0], 512 * bank[1], 512 * bank[1] + n)
+        w, ws, x, xs = V(q1 + "c", a1, a1 + 128), V(q1 + "s", a1, a1 + 128), V(q2 + "c", a2, a2 + n), V(q2 + "s", a2, a2 + n)
+        op("p", lambda: g.tensor.matmul_mx(o[0], w[0], ws[0], x[0], xs[0], True, True), [w, ws, x, xs], [o])
+        return o
+
+    def dst(c):
+        rid, pid = topo.addr(c)[:2]
+        return DstId(rid=rid, pnc=pid)
+
+    def engines(cs):
+        return sorted(set.intersection(*[set(topo.engines(core, c)) for c in cs]))
+
+    def send(outs, src, cs, sem):
+        e = engines(cs)
+        need("g", [src], [])
+        g.remote_dma_fused([RemoteDMATransfer(dst_ids=[dst(c) for c in cs], dma_engine_mask=sum(1 << k for k in e), remote_sem=T.sem[sem],
+                                              srcs=[src[0]], dsts=outs)], local_sem=T.sem.sent)
+        total["sent"] = total.get("sent", 0) + len(e)
+
+    def arrive(sem, n, views):
+        total[sem] = total.get(sem, 0) + n
+        for v in views:
+            hist.setdefault(v[1], []).append((v, True, sem, total[sem], {}, None))
+
+    def codes(name, a, b):
+        return T[name][:, a:b].bitcast(dt.uint8)
+
+    NW = [WIN[t][r][1] - WIN[t][r][0] for t in range(3)]
+    others = [c for c in T.cores if c != core]
+    ENG = len(engines(others))
+
+    def landpos(me, t):
+        return {k: i for i, k in enumerate([k for k, c in enumerate(CH[t]) if c[3] != me])}
+
+    dma("y", T.xt[:], T.x[:], "dx", [], [V("xt")])
+    dma("s", T.uin[:, 0:4], T.u[:, 0:4], "du", [], [V("uin", 0, 4)])
+    dma("y", T.at[:], T.a[:], "da", [], [V("at")])
+    dma("y", T.bt[:], T.b[:], "db", [], [V("bt")])
+    dma("y", T.wt[:], T.w[:], "dw", [], [V("wt")])
+
+    own0 = (P * r - WIN[0][r][0], P * r - WIN[0][r][0] + P)
+    nb = [s for s in (r - 1, r + 1) if 0 <= s < N]
+    wviews = []
+    for s in nb:
+        a, b = (0, own0[0]) if s < r else (own0[1], NW[0])
+        wviews += [V("r0c", a, b), V("r0s", a, b)]
+    arrive("arrw", 2 * ENG * len(nb), wviews)
+    for t in range(2):
+        arrive("arr%d" % t, 3 * ENG, [V("land%d" % t, 0, len(landpos(r, t)))])
+
+    ncol = max(len(landpos(r, 0)), len(landpos(r, 1)))
+    fill(V("uz"), 0.0)
+    fill(V("sp", 0, 128 * ncol), 0.0)
+    fill(V("carry", 0, 128 * ncol), 1.0)
+    fill(V("carry", 0, 128 * ncol, 32), 0.0)
+    for k in range(4):
+        ts(V("ut", k, 512, 4), V("uz"), V("uin", k, k + 1), None, Alu.add)
+    quant("u", 0, 128, V("ut"))
+    op("g", lambda: g.iota(T.pi[:, 0:1], [[0, 1]], 0, 1), [], [V("pi", 0, 1)])
+    for t in range(2):
+        op("g", lambda: g.iota(T["jt%d" % t][:, 0:6], [[64, 6]], WIN[t + 1][r][0], 1, allow_small_or_imprecise_dtypes=True), [], [V("jt%d" % t, 0, 6)])
+    fill(V("msp"), 0.0)
+    fill(V("carb"), 1.0)
+    fill(V("carb", 0, 640, 32), 0.0)
+    fill(V("ones"), 1.0)
+    quant("r0", own0[0], own0[1], V("xt"))
+
+    def score(t):
+        q = "r%d" % t
+        w0 = WIN[t][r][0]
+        mine = [c for c in CH[t] if c[3] == r]
+        n = len(mine)
+        for i, c in enumerate(mine):
+            mm(("psc", 1 + i), q, c[0] - w0, "u", 0, 128)
+        lo, hi = mine[0][0] + 32 * mine[0][1], mine[-1][0] + 32 * mine[-1][2]
+        o = mm(("psc", 0), "u", 0, q, lo - w0, hi - lo)
+        ow = V("own%d" % t, 0, n)
+        copy("v", ow, V("psc", 512, 512 * n + 1, 512))
+        outs = []
+        for c in others:
+            p = landpos(T.rank_of(c), t)[CH[t].index(mine[0])]
+            outs.append(T["land%d" % t][:, p:p + n])
+        send(outs, ow, others, "arr%d" % t)
+        copy("s", V("row%d" % t, lo, hi), o)
+
+    score(0)
+    for s in nb:
+        sw = WIN[0][s]
+        lo, hi = max(P * r, sw[0]), min(P * r + P, sw[1])
+        a, b = lo - WIN[0][r][0], hi - WIN[0][r][0]
+        c, d = lo - sw[0], hi - sw[0]
+        send([codes("r0c", c, d)], (codes("r0c", a, b),) + V("r0c", a, b)[1:], [T.cores[s]], "arrw")
+        send([T.r0s[:, c:d]], V("r0s", a, b), [T.cores[s]], "arrw")
+    for i in range(3):
+        op("g", lambda: g.iota(T.tn0[:, NW[0] * i:NW[0] * i + NW[0]], [[4, NW[0]]], 4 * WIN[0][r][0] + (2 if i == 2 else 0), 0, allow_small_or_imprecise_dtypes=True),
+           [], [V("tn0", NW[0] * i, NW[0] * i + NW[0])])
+
+    op("v", lambda: g.vector.tensor_scalar(T.pi[:, 1:2], T.pi[:, 0:1], 96, None, Alu.bitwise_and), [V("pi", 0, 1)], [V("pi", 1, 2)])
+    op("v", lambda: g.vector.tensor_scalar(T.pi[:, 2:3], T.pi[:, 0:1], 16, None, Alu.bitwise_and), [V("pi", 0, 1)], [V("pi", 2, 3)])
+    ts(V("dcol", 0, 1), V("pi", 1, 2), 0.5, None, Alu.mult)
+    tt(V("dcol", 1, 2), V("dcol", 0, 1), V("pi", 2, 3), Alu.add)
+
+    plan = []
+    for t in range(2):
+        a, b = NEED[t][r]
+        chunks = [k for k, c in enumerate(CH[t]) if c[0] + 32 * c[2] > a and c[0] + 32 * c[1] < b]
+        first = CH[t][chunks[0]][0] + 32 * CH[t][chunks[0]][1]
+        n = CH[t][chunks[-1]][0] + 32 * CH[t][chunks[-1]][2] - first
+        back = first > 0
+        segs = []
+        for i in range((NW[t + 1] + 63) // 64):
+            j0 = WIN[t + 1][r][0] + 64 * i
+            segs.append((max(j0 - 64, first), min(j0 + 66, first + n + 1)))
+        plan.append((chunks, first, n, back, segs))
+
+    def tables(t):
+        chunks, first, n, back, segs = plan[t]
+        W1, W2 = NW[t], 2 * NW[t]
+        m = len(segs)
+        h = m // 2
+        fill(V("fb%d" % t, 0, 1), float(first))
+        fill(V("cp%d" % t, 0, CW * h), 0.0)
+        fill(V("cp%d" % t, CW * h + CW - 1, CW * m, CW), 0.0)
+        for i, (lo, hi) in enumerate(segs):
+            w = hi - lo
+            if w < CW - 1:
+                fill(V("ca%d" % t, CW * i + w, CW * i + CW - 1), 0.0)
+                if i >= h:
+                    fill(V("cp%d" % t, CW * i + w, CW * i + CW - 1), 0.0)
+            fill(V("ca%d" % t, CW * i + CW - 1, CW * i + CW), float(lo - 1 - WIN[t][r][0] + W1 + W2 + W2 * w - (W1 * w if i < h else 0)))
+        fill(V("cum%d" % t, 0, 1), 0.0)
+        e = float(-K - LEN[t]) if back else 0.0
+        ts(V("jt%d" % t, 6, 12), V("jt%d" % t, 0, 6), V("dcol", 1, 2), e, Alu.subtract, Alu.add)
+        ts(V("jt%d" % t, 12, 18), V("jt%d" % t, 6, 12), 1.0, None, Alu.add)
+        ts(V("jt%d" % t, 18, 24), V("jt%d" % t, 6, 12), -1.0, None, Alu.mult)
+        ts(V("jt%d" % t, 24, 30), V("jt%d" % t, 6, 12), -1.0, -1.0, Alu.mult, Alu.add)
+
+    tables(0)
+    quant("a", 0, 512, V("at"))
+
+    def kids(t, qs, part):
+        q, w = "r%d" % t, NW[t]
+        for i in part:
+            o = mm(("pch", i % 4), "ab"[i // 4], 128 * (i % 4), q, 0, w)
+            h = V("h%s%d" % ("ab"[i // 4], t), i % 4, 4 * w, 4)
+            if qs[i] == "v":
+                ts(h, o, 0.0625, None, Alu.mult)
+            else:
+                act(h, o, Act.Copy, scale=0.0625)
+
+    def kidq(t, cuts):
+        q, w = "r%d" % t, NW[t]
+        cuts = [0] + cuts + [w]
+        return [lambda k=k, n=n, x=x, y=y: quant(q, k * w + x, k * w + y, V("%s%d" % (n, t), 4 * x, 4 * y))
+                for k, n in ((1, "ha"), (2, "hb")) for x, y in zip(cuts, cuts[1:])]
+
+    def fillin(jobs):
+        if jobs:
+            jobs.pop(0)()
+
+    def spread(src, n, name):
+        for b in range(4):
+            for a in range(4):
+                copy("vs"[(a + b) % 2], V(name, 32 * a, 128 * n, 128, 32 * b, 32 * b + 32), V(src, 0, n, 1, 32 * a, 32 * a + 32))
+
+    def runs(chs, base):
+        out = []
+        for i, c in enumerate(chs):
+            x, y, w = 128 * i + 32 * c[1], c[0] + 32 * c[1] - base, 32 * (c[2] - c[1])
+            if out and out[-1][0] + out[-1][2] == x and out[-1][1] + out[-1][2] == y:
+                out[-1] = (out[-1][0], out[-1][1], out[-1][2] + w)
+            else:
+                out.append((x, y, w))
+        return out
+
+    def order(t, nS, flight, hook1, hook2, hook3, jobs):
+        chunks, first, n, back, segs = plan[t]
+        L = LEN[t]
+        W = L + 128
+        lp = landpos(r, t)
+        nl = len(lp)
+        row, land = "row%d" % t, "land%d" % t
+        mine = [k for k, c in enumerate(CH[t]) if c[3] == r]
+        lo = CH[t][mine[0]][0] + 32 * CH[t][mine[0]][1]
+        hi = CH[t][mine[-1]][0] + 32 * CH[t][mine[-1]][2]
+        nV = len(chunks) - nS
+        v0 = nS if r % 2 else 0
+        onS = [i for i in range(len(chunks)) if not v0 <= i < v0 + nV]
+
+        def val(k):
+            return V(land, lp[k], lp[k] + 1) if k in lp else V("own%d" % t, k - mine[0], k - mine[0] + 1)
+
+        def equal(i):
+            s = CH[t][chunks[i]][0]
+            e = V("eq%d" % t, 128 * i, 128 * i + 128)
+            ts(e, V(row, s, s + 128), val(chunks[i]), None, Alu.is_equal)
+            d = V("cmp%d" % t, W * i + L, W * i + L + 128)
+            op("g", lambda: g.affine_select(d[0], e[0], [[-1, 128]], Alu.is_gt, 0.0, 0, 1), [e], [d])
+
+        def compare(i, a, b):
+            s = CH[t][chunks[i]][0]
+            for x, y, o in ((a, min(b, s), Alu.is_ge), (max(a, s), b, Alu.is_gt)):
+                if x < y:
+                    ts(V("cmp%d" % t, W * i + x, W * i + y), V(row, x, y), val(chunks[i]), None, o)
+
+        def count_of(i):
+            scan(V("so%d" % t, W // 2 * i, W // 2 * i + W // 2), V("cmp%d" % t, W * i, W * i + W // 2), V("cmp%d" % t, W * i + W // 2, W * i + W), 0.0, Alu.add, Alu.add)
+
+        early = [i for i in range(v0, v0 + nV) if chunks[i] in mine and lo <= CH[t][chunks[i]][0] and CH[t][chunks[i]][0] + 128 <= hi]
+        for i in early:
+            equal(i)
+            compare(i, lo, hi)
+        flight()
+        spread(land, nl, "sp")
+        scan(V("rep", 0, 128 * nl), V("carry", 0, 128 * nl), V("sp", 0, 128 * nl), 0.0, Alu.mult, Alu.add)
+        for i, x in enumerate(onS):
+            ts(V("neg%d" % t, i, i + 1), val(chunks[x]), -1.0, None, Alu.mult)
+        for x, y, w in runs([CH[t][k] for k in sorted(lp, key=lambda k: lp[k])], 0):
+            turn(V(row, y, y + w), V("rep", x, x + w))
+        hook1()
+        for i in range(len(chunks)):
+            if i not in early:
+                equal(i)
+        for i, c in enumerate(onS):
+            s = CH[t][chunks[c]][0]
+            o = 1088 * i
+            act(V("sg%d" % t, o, o + L), V(row, 0, L), Act.Sign, bias=V("neg%d" % t, i, i + 1))
+            if s:
+                act(V("sj%d" % t, o, o + s), V("sg%d" % t, o, o + s), Act.Relu, scale=-1.0, accum=V("acc%d" % t, 2 * i, 2 * i + 1))
+            act(V("sj%d" % t, o + s, o + L), V("sg%d" % t, o + s, o + L), Act.Relu, accum=V("acc%d" % t, 2 * i + 1, 2 * i + 2))
+        hook2()
+        for i in range(v0, v0 + nV):
+            if i in early:
+                compare(i, 0, lo)
+                compare(i, hi, L)
+            else:
+                compare(i, 0, L)
+            if i > v0:
+                count_of(i - 1)
+        for i, c in enumerate(onS):
+            d = V("cmp%d" % t, W * c + L, W * c + L + 128)
+            tr = V("tri%d" % t, i, i + 1)
+            op("v", lambda: g.vector.tensor_reduce(tr[0], d[0], AxisListType.X, Alu.add), [d], [tr])
+        count_of(v0 + nV - 1)
+        for i, c in enumerate(onS):
+            if CH[t][chunks[c]][0]:
+                ts(V("rho%d" % t, i, i + 1), V("acc%d" % t, 2 * i + 1, 2 * i + 2), V("acc%d" % t, 2 * i, 2 * i + 1), V("tri%d" % t, i, i + 1), Alu.subtract, Alu.add)
+            else:
+                tt(V("rho%d" % t, i, i + 1), V("acc%d" % t, 2 * i + 1, 2 * i + 2), V("tri%d" % t, i, i + 1), Alu.add)
+        ts(V("mk%d" % t, v0, v0 + nV), V("so%d" % t, W // 2 * v0 + W // 2 - 1, W // 2 * (v0 + nV), W // 2), float(K), None, Alu.is_lt)
+        for i, c in enumerate(onS):
+            ts(V("mk%d" % t, c, c + 1), V("rho%d" % t, i, i + 1), float(K - CH[t][chunks[c]][0]), None, Alu.is_lt)
+        nc = len(chunks)
+        spread("mk%d" % t, nc, "msp")
+        hook3()
+        fillin(jobs)
+        scan(V("mrep", 0, 128 * nc), V("carb", 0, 128 * nc), V("msp", 0, 128 * nc), 0.0, Alu.mult, Alu.add)
+        fillin(jobs)
+        for x, y, w in runs([CH[t][k] for k in chunks], first):
+            turn(V("mrow%d" % t, y, y + w), V("mrep", x, x + w))
+        fillin(jobs)
+        fb = "fb%d" % t
+        scan(V(fb, 1, n + 1), V("mrow%d" % t, 0, n), V("ones", 0, n), float(first), Alu.add, Alu.add)
+        fillin(jobs)
+        W1, W2 = NW[t], 2 * NW[t]
+        m = len(segs)
+        hm = m // 2
+        jj = "jt%d" % t
+        if back:
+            jj = "jj%d" % t
+            end = V(fb, n, n + 1)
+            ts(V(jj, 18, 30), V("jt%d" % t, 18, 30), end, None, Alu.subtract)
+            ts(V(jj, 6, 18), V("jt%d" % t, 6, 18), end, None, Alu.add)
+        for i, (a, b) in enumerate(segs):
+            f = V(fb, a - first, b - first)
+            w = b - a
+            act(V("fs%d" % t, CW * i, CW * i + w), f, Act.Sign, bias=V(jj, 18 + i, 19 + i), accum=V("sa%d" % t, i, i + 1))
+            ts(V("ca%d" % t, CW * i, CW * i + w), f, V(jj, 6 + i, 7 + i), float(1 + W1 - 2 * W2 + (W1 if i < hm else 0)), Alu.is_le, Alu.mult)
+            if i < hm:
+                act(V("fs%d" % t, CW * (6 + i), CW * (6 + i) + w), f, Act.Sign, bias=V(jj, 24 + i, 25 + i), accum=V("sb%d" % t, i, i + 1))
+            else:
+                ts(V("cp%d" % t, CW * i, CW * i + w), f, V(jj, 12 + i, 13 + i), float(-W1), Alu.is_le, Alu.mult)
+        scan(V("cum%d" % t, 1, 1 + m * CW), V("ca%d" % t, 0, m * CW), V("cp%d" % t, 0, m * CW), 0.0, Alu.add, Alu.add)
+        fillin(jobs)
+        ts(V("xa%d" % t, 0, m), V("sa%d" % t, 0, m), float(-W2), None, Alu.mult)
+        ts(V("xb%d" % t, 0, hm), V("sb%d" % t, 0, hm), float(W1), None, Alu.mult)
+        tt(V("dd%d" % t, 0, m), V("cum%d" % t, CW, m * CW + 1, CW), V("cum%d" % t, 0, (m - 1) * CW + 1, CW), Alu.subtract)
+        tt(V("xa%d" % t, 0, hm), V("xa%d" % t, 0, hm), V("xb%d" % t, 0, hm), Alu.add)
+        tt(V("ll%d" % t, 0, m), V("dd%d" % t, 0, m), V("xa%d" % t, 0, m), Alu.add)
+        for b in range(4):
+            for a in range(4):
+                copy("vs"[(a + b) % 2], V("wf%d" % t, a, 4 * m, 4, 32 * b, 32 * b + 32), V("ll%d" % t, 0, m, 1, 32 * a, 32 * a + 32))
+        while jobs:
+            fillin(jobs)
+        copy("v", V("wu%d" % t, 0, 4 * m), V("wf%d" % t, 0, 4 * m))
+
+    def pick(t):
+        n, w = NW[t + 1], 3 * NW[t]
+        off = V("wu%d" % t, 0, n // 16)
+        a, b = V("r%dc" % t, 0, w), V("r%dc" % (t + 1), 0, n)
+        op("v", lambda: g.vector.tensor_copy(b[0].bitcast(dt.uint32), a[0].bitcast(dt.uint32).indirect(off[0])), [a, off], [b])
+        c, d = V("r%ds" % t, 0, w), V("r%ds" % (t + 1), 0, n)
+        op("s", lambda: g.scalar.activation(d[0], c[0].indirect(off[0]), Act.Copy), [c, off], [d])
+
+    def numbers(t, out):
+        n, w = NW[t + 1], 3 * NW[t]
+        off, a = V("wu%d" % t, 0, n // 16), V("tn%d" % t, 0, w)
+        op("s", lambda: g.scalar.activation(out[0], a[0].indirect(off[0]), Act.Copy), [a, off], [out])
+
+    def nothing():
+        pass
+
+    def first_kids():
+        kids(0, "ssssssss", range(4))
+
+    def second_kids():
+        quant("b", 0, 512, V("bt"))
+        kids(0, "ssssssss", range(4, 8))
+    order(0, 1, nothing, first_kids, second_kids, nothing, kidq(0, [144, 288] if NW[0] > 400 else [144]))
+    pick(0)
+    score(1)
+
+    def all_kids():
+        kids(1, "vsvsvsvs", range(8))
+        tables(1)
+        quant("w", 0, 128, V("wt"))
+
+    def new_numbers():
+        numbers(0, V("tn1", 0, NW[1]))
+        copy("s", V("tn1", NW[1], 2 * NW[1]), V("tn1", 0, NW[1]))
+        act(V("tn1", 2 * NW[1], 3 * NW[1]), V("tn1", 0, NW[1]), Act.Identity, bias=1.0)
+    order(1, 2 if len(plan[1][0]) > 3 else 1, all_kids, nothing, nothing, new_numbers, kidq(1, [176] if NW[1] > 300 else [144]))
+    pick(1)
+    o = mm(("psc", 0), "w", 0, "r2", 0, E)
+    numbers(1, V("hsr"))
+    dma("y", T.oc[:], codes("r2c", 0, E), "out", [V("r2c")], [])
+    for k in range(4):
+        dma("y", T.osc[4 * k:4 * k + 4, :], T.r2s[32 * k:32 * k + 4, :], "out", [V("r2s")], [])
+    copy("v", V("ysb"), o)
+    dma("y", T.y[:], T.ysb[:], "out", [V("ysb")], [])
+    dma("s", T.hs[:], T.hsr[0:1, :], "out", [V("hsr")], [])
+    for s in sorted(total):
+        if known["g"].get(s, 0) < total[s]:
+            g.wait_ge(T.sem[s], total[s])

@@ -9,6 +9,7 @@ WIN = ([(0, 288), (160, 576), (448, 864), (736, 1024)], [(0, 288), (224, 576), (
 NEED = ([(0, 288), (0, 576), (448, 1024), (736, 1024)], [(0, 288), (0, 576), (512, 1088), (800, 1088)])
 F32, BF, I32, U16 = "float32", "bfloat16", "int32", "uint16"
 CW = 131
+HW = 66
 
 SCRATCH = {
     "xt": ("sbuf", [128, 1024], BF), "uin": ("sbuf", [128, 8], BF), "ut": ("sbuf", [128, 512], BF), "uz": ("sbuf", [128, 128], BF),
@@ -26,9 +27,9 @@ for _q, _n in (("u", 128), ("a", 512), ("b", 512), ("w", 128), ("r0", 1248), ("r
 for _t in range(2):
     for _n, _w, _d in (("ha", 1664, BF), ("hb", 1664, BF), ("row", 1088, F32), ("own", 4, F32), ("land", 8, F32), ("cmp", 5 * 1216, BF),
                        ("eq", 640, BF), ("sg", 2 * 1088, BF), ("sj", 2 * 1088, BF), ("so", 5 * 608, BF), ("neg", 2, F32), ("acc", 4, F32), ("tri", 2, F32),
-                       ("rho", 2, F32), ("mk", 5, F32), ("mrow", 640, BF), ("fb", 644, F32), ("ca", 6 * CW, F32), ("cp", 6 * CW, F32), ("cum", 6 * CW + 4, F32),
-                       ("jt", 30, F32), ("jj", 30, F32), ("fs", 12 * CW, BF), ("sa", 6, F32), ("sb", 6, F32), ("xa", 6, F32), ("xb", 6, F32),
-                       ("dd", 6, F32), ("ll", 6, F32), ("wf", 24, F32), ("wu", 24, U16)):
+                       ("rho", 2, F32), ("mk", 5, F32), ("mrow", 640, BF), ("fb", 644, F32), ("ch", 12 * HW, F32), ("ca", 3 * CW, F32), ("cp", 3 * CW, F32),
+                       ("cuh", 6 * HW + 4, F32), ("cum", 3 * CW + 4, F32), ("jt", 18, F32), ("jj", 18, F32), ("fs", 12 * CW, BF), ("sa", 6, F32), ("sb", 6, F32),
+                       ("xa", 6, F32), ("xb", 6, F32), ("dd", 6, F32), ("ll", 6, F32), ("wf", 24, F32), ("wu", 24, U16)):
         SCRATCH["%s%d" % (_n, _t)] = ("sbuf", [128, _w], _d)
 SEMAPHORES = ["v", "s", "p", "gc", "sent", "arr0", "arr1", "arrw", "dx", "du", "da", "db", "dw", "out"]
 
@@ -179,21 +180,72 @@ def rank_program(g, core, T, topo):
     for t in range(2):
         arrive("arr%d" % t, 3 * ENG, [V("land%d" % t, 0, len(landpos(r, t)))])
 
+    plan = []
+    for t in range(2):
+        a, b = NEED[t][r]
+        chunks = [k for k, c in enumerate(CH[t]) if c[0] + 32 * c[2] > a and c[0] + 32 * c[1] < b]
+        back = a > 0
+        segs = []
+        for i in range((NW[t + 1] + 63) // 64):
+            j0 = WIN[t + 1][r][0] + 64 * i
+            segs.append((max(j0 - 64, a), min(j0 + 66, b + 1)))
+        plan.append((chunks, a, b - a, back, segs))
+
     ncol = max(len(landpos(r, 0)), len(landpos(r, 1)))
     fill(V("uz"), 0.0)
-    fill(V("sp", 0, 128 * ncol), 0.0)
+    op("g", lambda: g.iota(T.pi[:, 0:1], [[0, 1]], 0, 1), [], [V("pi", 0, 1)])
+    for t in range(2):
+        e = -K - LEN[t] if plan[t][3] else 0
+        op("g", lambda: g.iota(T["jt%d" % t][:, 0:6], [[64, 6]], WIN[t + 1][r][0] + e, 1, allow_small_or_imprecise_dtypes=True), [], [V("jt%d" % t, 0, 6)])
+    op("g", lambda: g.iota(T.sp[:, 0:128 * ncol], [[0, 128 * ncol]], 0, 0, allow_small_or_imprecise_dtypes=True), [], [V("sp", 0, 128 * ncol)])
     fill(V("carry", 0, 128 * ncol), 1.0)
     fill(V("carry", 0, 128 * ncol, 32), 0.0)
+    op("v", lambda: g.vector.tensor_scalar(T.pi[:, 1:2], T.pi[:, 0:1], 96, None, Alu.bitwise_and), [V("pi", 0, 1)], [V("pi", 1, 2)])
+    op("v", lambda: g.vector.tensor_scalar(T.pi[:, 2:3], T.pi[:, 0:1], 16, None, Alu.bitwise_and), [V("pi", 0, 1)], [V("pi", 2, 3)])
+    fill(V("msp"), 0.0)
+    ts(V("dcol", 0, 1), V("pi", 1, 2), -0.5, None, Alu.mult)
+    fill(V("carb"), 1.0)
+    tt(V("dcol", 1, 2), V("dcol", 0, 1), V("pi", 2, 3), Alu.subtract)
+    fill(V("carb", 0, 640, 32), 0.0)
+    fill(V("ones"), 1.0)
+
+    def tables(t, q):
+        chunks, first, n, back, segs = plan[t]
+        W1, W2 = NW[t], 2 * NW[t]
+        m = len(segs)
+        h = (m + 2) // 2
+
+        def put(out, c):
+            if q == "v":
+                fill(out, c)
+            else:
+                act(out, V("uz", 0, out[3] - out[2]), Act.Identity, bias=c)
+        put(V("fb%d" % t, 0, 1), float(first))
+        put(V("cuh%d" % t, 0, 1), 0.0)
+        put(V("cum%d" % t, 0, 1), 0.0)
+        for i, (lo, hi) in enumerate(segs):
+            w = hi - lo
+            c = float(lo - 1 - WIN[t][r][0] + W1 + W2 + W2 * w - (W1 * w if i < h else 0))
+            if i < h:
+                put(V("ch%d" % t, 2 * HW * i + w, 2 * HW * (i + 1)), 0.0)
+                put(V("ch%d" % t, 2 * HW * i + 2 * HW - 1, 2 * HW * (i + 1)), c)
+            else:
+                o = CW * (i - h)
+                put(V("ca%d" % t, o + w, o + CW), c if w == CW - 1 else 0.0)
+                put(V("cp%d" % t, o + w, o + CW), 0.0)
+                if w < CW - 1:
+                    put(V("ca%d" % t, o + CW - 1, o + CW), c)
+        if q == "v":
+            ts(V("jt%d" % t, 6, 12), V("jt%d" % t, 0, 6), V("dcol", 1, 2), None, Alu.add)
+            ts(V("jt%d" % t, 12, 18), V("jt%d" % t, 0, 6), V("dcol", 1, 2), 1.0, Alu.add, Alu.add)
+        else:
+            act(V("jt%d" % t, 6, 12), V("jt%d" % t, 0, 6), Act.Identity, bias=V("dcol", 1, 2))
+            act(V("jt%d" % t, 12, 18), V("jt%d" % t, 6, 12), Act.Identity, bias=1.0)
+
+    tables(0, "s")
     for k in range(4):
         ts(V("ut", k, 512, 4), V("uz"), V("uin", k, k + 1), None, Alu.add)
     quant("u", 0, 128, V("ut"))
-    op("g", lambda: g.iota(T.pi[:, 0:1], [[0, 1]], 0, 1), [], [V("pi", 0, 1)])
-    for t in range(2):
-        op("g", lambda: g.iota(T["jt%d" % t][:, 0:6], [[64, 6]], WIN[t + 1][r][0], 1, allow_small_or_imprecise_dtypes=True), [], [V("jt%d" % t, 0, 6)])
-    fill(V("msp"), 0.0)
-    fill(V("carb"), 1.0)
-    fill(V("carb", 0, 640, 32), 0.0)
-    fill(V("ones"), 1.0)
     quant("r0", own0[0], own0[1], V("xt"))
 
     def score(t):
@@ -225,65 +277,30 @@ def rank_program(g, core, T, topo):
     for i in range(3):
         op("g", lambda: g.iota(T.tn0[:, NW[0] * i:NW[0] * i + NW[0]], [[4, NW[0]]], 4 * WIN[0][r][0] + (2 if i == 2 else 0), 0, allow_small_or_imprecise_dtypes=True),
            [], [V("tn0", NW[0] * i, NW[0] * i + NW[0])])
+    bank = [0]
 
-    op("v", lambda: g.vector.tensor_scalar(T.pi[:, 1:2], T.pi[:, 0:1], 96, None, Alu.bitwise_and), [V("pi", 0, 1)], [V("pi", 1, 2)])
-    op("v", lambda: g.vector.tensor_scalar(T.pi[:, 2:3], T.pi[:, 0:1], 16, None, Alu.bitwise_and), [V("pi", 0, 1)], [V("pi", 2, 3)])
-    ts(V("dcol", 0, 1), V("pi", 1, 2), 0.5, None, Alu.mult)
-    tt(V("dcol", 1, 2), V("dcol", 0, 1), V("pi", 2, 3), Alu.add)
-
-    plan = []
-    for t in range(2):
-        a, b = NEED[t][r]
-        chunks = [k for k, c in enumerate(CH[t]) if c[0] + 32 * c[2] > a and c[0] + 32 * c[1] < b]
-        first = CH[t][chunks[0]][0] + 32 * CH[t][chunks[0]][1]
-        n = CH[t][chunks[-1]][0] + 32 * CH[t][chunks[-1]][2] - first
-        back = first > 0
-        segs = []
-        for i in range((NW[t + 1] + 63) // 64):
-            j0 = WIN[t + 1][r][0] + 64 * i
-            segs.append((max(j0 - 64, first), min(j0 + 66, first + n + 1)))
-        plan.append((chunks, first, n, back, segs))
-
-    def tables(t):
-        chunks, first, n, back, segs = plan[t]
-        W1, W2 = NW[t], 2 * NW[t]
-        m = len(segs)
-        h = m // 2
-        fill(V("fb%d" % t, 0, 1), float(first))
-        fill(V("cp%d" % t, 0, CW * h), 0.0)
-        fill(V("cp%d" % t, CW * h + CW - 1, CW * m, CW), 0.0)
-        for i, (lo, hi) in enumerate(segs):
-            w = hi - lo
-            if w < CW - 1:
-                fill(V("ca%d" % t, CW * i + w, CW * i + CW - 1), 0.0)
-                if i >= h:
-                    fill(V("cp%d" % t, CW * i + w, CW * i + CW - 1), 0.0)
-            fill(V("ca%d" % t, CW * i + CW - 1, CW * i + CW), float(lo - 1 - WIN[t][r][0] + W1 + W2 + W2 * w - (W1 * w if i < h else 0)))
-        fill(V("cum%d" % t, 0, 1), 0.0)
-        e = float(-K - LEN[t]) if back else 0.0
-        ts(V("jt%d" % t, 6, 12), V("jt%d" % t, 0, 6), V("dcol", 1, 2), e, Alu.subtract, Alu.add)
-        ts(V("jt%d" % t, 12, 18), V("jt%d" % t, 6, 12), 1.0, None, Alu.add)
-        ts(V("jt%d" % t, 18, 24), V("jt%d" % t, 6, 12), -1.0, None, Alu.mult)
-        ts(V("jt%d" % t, 24, 30), V("jt%d" % t, 6, 12), -1.0, -1.0, Alu.mult, Alu.add)
-
-    tables(0)
-    quant("a", 0, 512, V("at"))
-
-    def kids(t, qs, part):
+    def kids(t, qs, part, cols=None):
         q, w = "r%d" % t, NW[t]
+        cols = cols or [(0, w)]
+        lo, hi = cols[0][0], cols[-1][1]
+        m0 = max(0, min(lo, hi - 128))
+        n = max(hi, m0 + 128) - m0
         for i in part:
-            o = mm(("pch", i % 4), "ab"[i // 4], 128 * (i % 4), q, 0, w)
-            h = V("h%s%d" % ("ab"[i // 4], t), i % 4, 4 * w, 4)
-            if qs[i] == "v":
-                ts(h, o, 0.0625, None, Alu.mult)
-            else:
-                act(h, o, Act.Copy, scale=0.0625)
+            buf, k = ("pch", "psc")[bank[0] // 4 % 2], bank[0] % 4
+            bank[0] += 1
+            mm((buf, k), "ab"[i // 4], 128 * (i % 4), q, m0, n)
+            for x, y in cols:
+                o = V(buf, 512 * k + x - m0, 512 * k + y - m0)
+                h = V("h%s%d" % ("ab"[i // 4], t), 4 * x + i % 4, 4 * y, 4)
+                if qs[i] == "v":
+                    ts(h, o, 0.0625, None, Alu.mult)
+                else:
+                    act(h, o, Act.Copy, scale=0.0625)
 
-    def kidq(t, cuts):
+    def kidq(t, cuts, seq):
         q, w = "r%d" % t, NW[t]
         cuts = [0] + cuts + [w]
-        return [lambda k=k, n=n, x=x, y=y: quant(q, k * w + x, k * w + y, V("%s%d" % (n, t), 4 * x, 4 * y))
-                for k, n in ((1, "ha"), (2, "hb")) for x, y in zip(cuts, cuts[1:])]
+        return [lambda k=k, x=cuts[i], y=cuts[i + 1]: quant(q, (k + 1) * w + x, (k + 1) * w + y, V("h%s%d" % ("ab"[k], t), 4 * x, 4 * y)) for k, i in seq]
 
     def fillin(jobs):
         if jobs:
@@ -294,17 +311,18 @@ def rank_program(g, core, T, topo):
             for a in range(4):
                 copy("vs"[(a + b) % 2], V(name, 32 * a, 128 * n, 128, 32 * b, 32 * b + 32), V(src, 0, n, 1, 32 * a, 32 * a + 32))
 
-    def runs(chs, base):
+    def runs(chs, base, size):
         out = []
         for i, c in enumerate(chs):
-            x, y, w = 128 * i + 32 * c[1], c[0] + 32 * c[1] - base, 32 * (c[2] - c[1])
+            lo, hi = max(c[0] + 32 * c[1], base), min(c[0] + 32 * c[2], base + size)
+            x, y, w = 128 * i + lo - c[0], lo - base, hi - lo
             if out and out[-1][0] + out[-1][2] == x and out[-1][1] + out[-1][2] == y:
                 out[-1] = (out[-1][0], out[-1][1], out[-1][2] + w)
             else:
                 out.append((x, y, w))
         return out
 
-    def order(t, nS, flight, hook1, hook2, hook3, jobs):
+    def order(t, nS, flight, hook1, hook2, jobs):
         chunks, first, n, back, segs = plan[t]
         L = LEN[t]
         W = L + 128
@@ -345,8 +363,8 @@ def rank_program(g, core, T, topo):
         spread(land, nl, "sp")
         scan(V("rep", 0, 128 * nl), V("carry", 0, 128 * nl), V("sp", 0, 128 * nl), 0.0, Alu.mult, Alu.add)
         for i, x in enumerate(onS):
-            ts(V("neg%d" % t, i, i + 1), val(chunks[x]), -1.0, None, Alu.mult)
-        for x, y, w in runs([CH[t][k] for k in sorted(lp, key=lambda k: lp[k])], 0):
+            act(V("neg%d" % t, i, i + 1), val(chunks[x]), Act.Copy, scale=-1.0)
+        for x, y, w in runs([CH[t][k] for k in sorted(lp, key=lambda k: lp[k])], 0, L):
             turn(V(row, y, y + w), V("rep", x, x + w))
         hook1()
         for i in range(len(chunks)):
@@ -359,7 +377,6 @@ def rank_program(g, core, T, topo):
             if s:
                 act(V("sj%d" % t, o, o + s), V("sg%d" % t, o, o + s), Act.Relu, scale=-1.0, accum=V("acc%d" % t, 2 * i, 2 * i + 1))
             act(V("sj%d" % t, o + s, o + L), V("sg%d" % t, o + s, o + L), Act.Relu, accum=V("acc%d" % t, 2 * i + 1, 2 * i + 2))
-        hook2()
         for i in range(v0, v0 + nV):
             if i in early:
                 compare(i, 0, lo)
@@ -381,13 +398,14 @@ def rank_program(g, core, T, topo):
         ts(V("mk%d" % t, v0, v0 + nV), V("so%d" % t, W // 2 * v0 + W // 2 - 1, W // 2 * (v0 + nV), W // 2), float(K), None, Alu.is_lt)
         for i, c in enumerate(onS):
             ts(V("mk%d" % t, c, c + 1), V("rho%d" % t, i, i + 1), float(K - CH[t][chunks[c]][0]), None, Alu.is_lt)
-        nc = len(chunks)
-        spread("mk%d" % t, nc, "msp")
-        hook3()
+        spread("mk%d" % t, len(chunks), "msp")
+        hook2()
         fillin(jobs)
-        scan(V("mrep", 0, 128 * nc), V("carb", 0, 128 * nc), V("msp", 0, 128 * nc), 0.0, Alu.mult, Alu.add)
+        pieces = runs([CH[t][k] for k in chunks], first, n)
+        x0, x1 = pieces[0][0], pieces[-1][0] + pieces[-1][2]
+        scan(V("mrep", x0, x1), V("carb", x0, x1), V("msp", x0, x1), 0.0, Alu.mult, Alu.add)
         fillin(jobs)
-        for x, y, w in runs([CH[t][k] for k in chunks], first):
+        for x, y, w in pieces:
             turn(V("mrow%d" % t, y, y + w), V("mrep", x, x + w))
         fillin(jobs)
         fb = "fb%d" % t
@@ -395,27 +413,31 @@ def rank_program(g, core, T, topo):
         fillin(jobs)
         W1, W2 = NW[t], 2 * NW[t]
         m = len(segs)
-        hm = m // 2
+        hm = (m + 2) // 2
+        z = m - hm
         jj = "jt%d" % t
         if back:
             jj = "jj%d" % t
-            end = V(fb, n, n + 1)
-            ts(V(jj, 18, 30), V("jt%d" % t, 18, 30), end, None, Alu.subtract)
-            ts(V(jj, 6, 18), V("jt%d" % t, 6, 18), end, None, Alu.add)
+            ts(V(jj, 6, 18), V("jt%d" % t, 6, 18), V(fb, n, n + 1), None, Alu.add)
         for i, (a, b) in enumerate(segs):
             f = V(fb, a - first, b - first)
             w = b - a
-            act(V("fs%d" % t, CW * i, CW * i + w), f, Act.Sign, bias=V(jj, 18 + i, 19 + i), accum=V("sa%d" % t, i, i + 1))
-            ts(V("ca%d" % t, CW * i, CW * i + w), f, V(jj, 6 + i, 7 + i), float(1 + W1 - 2 * W2 + (W1 if i < hm else 0)), Alu.is_le, Alu.mult)
+            c = float(1 + W1 - 2 * W2 + (W1 if i < hm else 0))
+            act(V("fs%d" % t, CW * i, CW * i + w), f, Act.Sign, bias=V(jj, 6 + i, 7 + i), scale=-1.0, accum=V("sa%d" % t, i, i + 1))
             if i < hm:
-                act(V("fs%d" % t, CW * (6 + i), CW * (6 + i) + w), f, Act.Sign, bias=V(jj, 24 + i, 25 + i), accum=V("sb%d" % t, i, i + 1))
+                act(V("fs%d" % t, CW * (6 + i), CW * (6 + i) + w), f, Act.Sign, bias=V(jj, 12 + i, 13 + i), scale=-1.0, accum=V("sb%d" % t, i, i + 1))
+                ts(V("ch%d" % t, 2 * HW * i, 2 * HW * i + w), f, V(jj, 6 + i, 7 + i), c, Alu.is_le, Alu.mult)
             else:
-                ts(V("cp%d" % t, CW * i, CW * i + w), f, V(jj, 12 + i, 13 + i), float(-W1), Alu.is_le, Alu.mult)
-        scan(V("cum%d" % t, 1, 1 + m * CW), V("ca%d" % t, 0, m * CW), V("cp%d" % t, 0, m * CW), 0.0, Alu.add, Alu.add)
+                o = CW * (i - hm)
+                ts(V("ca%d" % t, o, o + w), f, V(jj, 6 + i, 7 + i), c, Alu.is_le, Alu.mult)
+                ts(V("cp%d" % t, o, o + w), f, V(jj, 12 + i, 13 + i), float(-W1), Alu.is_le, Alu.mult)
+        scan(V("cuh%d" % t, 1, 1 + hm * HW), V("ch%d" % t, 0, 2 * hm * HW, 2), V("ch%d" % t, 1, 2 * hm * HW, 2), 0.0, Alu.add, Alu.add)
+        scan(V("cum%d" % t, 1, 1 + z * CW), V("ca%d" % t, 0, z * CW), V("cp%d" % t, 0, z * CW), 0.0, Alu.add, Alu.add)
         fillin(jobs)
-        ts(V("xa%d" % t, 0, m), V("sa%d" % t, 0, m), float(-W2), None, Alu.mult)
-        ts(V("xb%d" % t, 0, hm), V("sb%d" % t, 0, hm), float(W1), None, Alu.mult)
-        tt(V("dd%d" % t, 0, m), V("cum%d" % t, CW, m * CW + 1, CW), V("cum%d" % t, 0, (m - 1) * CW + 1, CW), Alu.subtract)
+        tt(V("dd%d" % t, 0, hm), V("cuh%d" % t, HW, hm * HW + 1, HW), V("cuh%d" % t, 0, (hm - 1) * HW + 1, HW), Alu.subtract)
+        ts(V("xa%d" % t, 0, m), V("sa%d" % t, 0, m), float(W2), None, Alu.mult)
+        ts(V("xb%d" % t, 0, hm), V("sb%d" % t, 0, hm), float(-W1), None, Alu.mult)
+        tt(V("dd%d" % t, hm, m), V("cum%d" % t, CW, z * CW + 1, CW), V("cum%d" % t, 0, (z - 1) * CW + 1, CW), Alu.subtract)
         tt(V("xa%d" % t, 0, hm), V("xa%d" % t, 0, hm), V("xb%d" % t, 0, hm), Alu.add)
         tt(V("ll%d" % t, 0, m), V("dd%d" % t, 0, m), V("xa%d" % t, 0, m), Alu.add)
         for b in range(4):
@@ -425,12 +447,12 @@ def rank_program(g, core, T, topo):
             fillin(jobs)
         copy("v", V("wu%d" % t, 0, 4 * m), V("wf%d" % t, 0, 4 * m))
 
-    def pick(t):
-        n, w = NW[t + 1], 3 * NW[t]
-        off = V("wu%d" % t, 0, n // 16)
-        a, b = V("r%dc" % t, 0, w), V("r%dc" % (t + 1), 0, n)
+    def pick(t, x=0, y=None):
+        y, w = y or NW[t + 1], 3 * NW[t]
+        off = V("wu%d" % t, x // 16, y // 16)
+        a, b = V("r%dc" % t, 0, w), V("r%dc" % (t + 1), x, y)
         op("v", lambda: g.vector.tensor_copy(b[0].bitcast(dt.uint32), a[0].bitcast(dt.uint32).indirect(off[0])), [a, off], [b])
-        c, d = V("r%ds" % t, 0, w), V("r%ds" % (t + 1), 0, n)
+        c, d = V("r%ds" % t, 0, w), V("r%ds" % (t + 1), x, y)
         op("s", lambda: g.scalar.activation(d[0], c[0].indirect(off[0]), Act.Copy), [c, off], [d])
 
     def numbers(t, out):
@@ -438,38 +460,58 @@ def rank_program(g, core, T, topo):
         off, a = V("wu%d" % t, 0, n // 16), V("tn%d" % t, 0, w)
         op("s", lambda: g.scalar.activation(out[0], a[0].indirect(off[0]), Act.Copy), [a, off], [out])
 
-    def nothing():
-        pass
+    border = [(0, own0[0])] * (own0[0] > 0) + [(own0[1], NW[0])] * (own0[1] < NW[0])
 
-    def first_kids():
-        kids(0, "ssssssss", range(4))
-
-    def second_kids():
+    def own_first_kids():
+        quant("a", 0, 512, V("at"))
+        kids(0, "ssssssss", range(4), [own0])
         quant("b", 0, 512, V("bt"))
-        kids(0, "ssssssss", range(4, 8))
-    order(0, 1, nothing, first_kids, second_kids, nothing, kidq(0, [144, 288] if NW[0] > 400 else [144]))
+
+    def own_second_kids():
+        kids(0, "ssssssss", range(4, 8), [own0])
+
+    def border_kids():
+        kids(0, "ssssssss", range(8), border)
+    if len(border) == 2:
+        jobs = kidq(0, [144, 288], [(0, 1), (1, 1), (0, 0), (0, 2), (1, 0), (1, 2)])
+    else:
+        own, edge = (0, 1) if r == 0 else (1, 0)
+        jobs = kidq(0, [144], [(0, own), (1, own), (0, edge), (1, edge)])
+    order(0, 2 if len(plan[0][0]) > 3 else 1, own_first_kids, own_second_kids, border_kids, jobs)
     pick(0)
     score(1)
 
-    def all_kids():
-        kids(1, "vsvsvsvs", range(8))
-        tables(1)
+    def first_kids():
+        kids(1, "vsvsssss", range(4))
+        tables(1, "v")
         quant("w", 0, 128, V("wt"))
+        kidq(1, [], [(0, 0)])[0]()
+
+    def second_kids():
+        kids(1, "vsvsssss", range(4, 8))
 
     def new_numbers():
         numbers(0, V("tn1", 0, NW[1]))
         copy("s", V("tn1", NW[1], 2 * NW[1]), V("tn1", 0, NW[1]))
         act(V("tn1", 2 * NW[1], 3 * NW[1]), V("tn1", 0, NW[1]), Act.Identity, bias=1.0)
-    order(1, 2 if len(plan[1][0]) > 3 else 1, all_kids, nothing, nothing, new_numbers, kidq(1, [176] if NW[1] > 300 else [144]))
-    pick(1)
-    o = mm(("psc", 0), "w", 0, "r2", 0, E)
+    order(1, 2 if len(plan[1][0]) > 3 else 1, first_kids, second_kids, new_numbers, kidq(1, [176 if NW[1] > 300 else 144], [(1, 0), (1, 1)]))
+    cut = ((0, 160), (160, E))
+    for x, y in cut:
+        pick(1, x, y)
+    outs = [mm(("psc", i), "w", 0, "r2", x, y - x) for i, (x, y) in enumerate(cut)]
     numbers(1, V("hsr"))
+
+    def scales(q, k):
+        dma(q, T.osc[4 * k:4 * k + 4, :], T.r2s[32 * k:32 * k + 4, :], "out", [V("r2s")], [])
     dma("y", T.oc[:], codes("r2c", 0, E), "out", [V("r2c")], [])
-    for k in range(4):
-        dma("y", T.osc[4 * k:4 * k + 4, :], T.r2s[32 * k:32 * k + 4, :], "out", [V("r2s")], [])
-    copy("v", V("ysb"), o)
-    dma("y", T.y[:], T.ysb[:], "out", [V("ysb")], [])
+    scales("y", 0)
+    scales("y", 1)
     dma("s", T.hs[:], T.hsr[0:1, :], "out", [V("hsr")], [])
+    scales("s", 2)
+    scales("s", 3)
+    for o, (x, y) in zip(outs, cut):
+        copy("v", V("ysb", x, y), o)
+    dma("y", T.y[:], T.ysb[:], "out", [V("ysb")], [])
     for s in sorted(total):
         if known["g"].get(s, 0) < total[s]:
             g.wait_ge(T.sem[s], total[s])

@@ -10,11 +10,11 @@ NEED = ([(0, 288), (0, 576), (448, 1024), (736, 1024)], [(0, 288), (0, 576), (51
 F32, BF, I32, U16 = "float32", "bfloat16", "int32", "uint16"
 CW = 131
 HW = 66
+CMPW = 448
 
 SCRATCH = {
     "xt": ("sbuf", [128, 1024], BF), "uin": ("sbuf", [128, 8], BF), "ut": ("sbuf", [128, 512], BF), "uz": ("sbuf", [128, 128], BF),
     "at": ("sbuf", [128, 2048], BF), "bt": ("sbuf", [128, 2048], BF), "wt": ("sbuf", [128, 512], BF),
-    "sp": ("sbuf", [128, 1024], F32), "rep": ("sbuf", [128, 1024], F32), "carry": ("sbuf", [128, 1024], F32),
     "msp": ("sbuf", [128, 640], BF), "mrep": ("sbuf", [128, 640], BF), "ones": ("sbuf", [128, 640], BF), "carb": ("sbuf", [128, 640], BF),
     "pi": ("sbuf", [128, 4], I32), "dcol": ("sbuf", [128, 2], F32),
     "psc": ("psum", [128, 2048], F32), "pch": ("psum", [128, 2048], F32),
@@ -25,13 +25,14 @@ for _q, _n in (("u", 128), ("a", 512), ("b", 512), ("w", 128), ("r0", 1248), ("r
     SCRATCH[_q + "c"] = ("sbuf", [128, _n], "float8_e4m3fn_x4")
     SCRATCH[_q + "s"] = ("sbuf", [128, _n], "uint8")
 for _t in range(2):
-    for _n, _w, _d in (("ha", 1664, BF), ("hb", 1664, BF), ("row", 1088, F32), ("own", 4, F32), ("land", 8, F32), ("cmp", 5 * 1216, BF),
-                       ("eq", 640, BF), ("sg", 2 * 1088, BF), ("sj", 2 * 1088, BF), ("so", 5 * 608, BF), ("neg", 2, F32), ("acc", 4, F32), ("tri", 2, F32),
-                       ("rho", 2, F32), ("mk", 5, F32), ("mrow", 640, BF), ("fb", 644, F32), ("ch", 12 * HW, F32), ("ca", 3 * CW, F32), ("cp", 3 * CW, F32),
+    for _n, _w, _d in (("ha", 1664, BF), ("hb", 1664, BF), ("own", 4, F32), ("land", 8, F32), ("cmp", 9 * CMPW, BF),
+                       ("eq", 384, BF), ("sg", 3 * 320, BF), ("sj", 3 * 320, BF), ("so", 9 * CMPW // 2, BF), ("acc", 3, F32),
+                       ("part", 9, BF), ("pland", 16, BF), ("rho", 15, F32), ("mk", 5, F32), ("mrow", 640, BF), ("fb", 644, F32),
+                       ("ch", 12 * HW, F32), ("ca", 3 * CW, F32), ("cp", 3 * CW, F32),
                        ("cuh", 6 * HW + 4, F32), ("cum", 3 * CW + 4, F32), ("jt", 18, F32), ("jj", 18, F32), ("fs", 12 * CW, BF), ("sa", 6, F32), ("sb", 6, F32),
                        ("xa", 6, F32), ("xb", 6, F32), ("dd", 6, F32), ("ll", 6, F32), ("wf", 24, F32), ("wu", 24, U16)):
         SCRATCH["%s%d" % (_n, _t)] = ("sbuf", [128, _w], _d)
-SEMAPHORES = ["v", "s", "p", "gc", "sent", "arr0", "arr1", "arrw", "dx", "du", "da", "db", "dw", "out"]
+SEMAPHORES = ["v", "s", "p", "gc", "sent", "arrw", "dx0", "dx1", "du", "da", "db", "dw", "out"] + ["%s%d_%d" % (k, t, r) for k in ("arr", "cnt") for t in range(2) for r in range(N)]
 
 
 def rank_program(g, core, T, topo):
@@ -149,6 +150,14 @@ def rank_program(g, core, T, topo):
                                               srcs=[src[0]], dsts=outs)], local_sem=T.sem.sent)
         total["sent"] = total.get("sent", 0) + len(e)
 
+    def send_halves(jobs, sem):
+        e = engines(others)
+        h = len(e) // 2
+        need("g", [j[1] for j in jobs], [])
+        g.remote_dma_fused([RemoteDMATransfer(dst_ids=[dst(c) for c in cs], dma_engine_mask=sum(1 << k for k in e[h * i:h * i + h]), remote_sem=T.sem[sem],
+                                              srcs=[src[0]], dsts=outs) for i, (outs, src, cs) in enumerate(jobs)], local_sem=T.sem.sent)
+        total["sent"] = total.get("sent", 0) + 2 * h
+
     def arrive(sem, n, views):
         total[sem] = total.get(sem, 0) + n
         for v in views:
@@ -159,12 +168,21 @@ def rank_program(g, core, T, topo):
 
     NW = [WIN[t][r][1] - WIN[t][r][0] for t in range(3)]
     others = [c for c in T.cores if c != core]
+    others_r = [T.rank_of(c) for c in others]
     ENG = len(engines(others))
+    half = (T.cores[:N // 2], T.cores[N // 2:])
+
+    def slot(me, s):
+        return s if s < me else s - 1
+
+    def group(me, t):
+        return list(range(5)) if me < N // 2 else list(range(len(CH[t]) - 5, len(CH[t])))
 
     def landpos(me, t):
         return {k: i for i, k in enumerate([k for k, c in enumerate(CH[t]) if c[3] != me])}
 
-    dma("y", T.xt[:], T.x[:], "dx", [], [V("xt")])
+    for i in range(2):
+        dma("y", T.xt[:, 512 * i:512 * i + 512], T.x[:, 512 * i:512 * i + 512], "dx%d" % i, [], [V("xt", 512 * i, 512 * i + 512)])
     dma("s", T.uin[:, 0:4], T.u[:, 0:4], "du", [], [V("uin", 0, 4)])
     dma("y", T.at[:], T.a[:], "da", [], [V("at")])
     dma("y", T.bt[:], T.b[:], "db", [], [V("bt")])
@@ -178,7 +196,10 @@ def rank_program(g, core, T, topo):
         wviews += [V("r0c", a, b), V("r0s", a, b)]
     arrive("arrw", 2 * ENG * len(nb), wviews)
     for t in range(2):
-        arrive("arr%d" % t, 3 * ENG, [V("land%d" % t, 0, len(landpos(r, t)))])
+        for s in others_r:
+            cols = [landpos(r, t)[k] for k, c in enumerate(CH[t]) if c[3] == s]
+            arrive("arr%d_%d" % (t, s), ENG, [V("land%d" % t, cols[0], cols[-1] + 1)])
+            arrive("cnt%d_%d" % (t, s), ENG // 2, [V("pland%d" % t, 5 * slot(r, s), 5 * slot(r, s) + 5)])
 
     plan = []
     for t in range(2):
@@ -191,62 +212,52 @@ def rank_program(g, core, T, topo):
             segs.append((max(j0 - 64, a), min(j0 + 66, b + 1)))
         plan.append((chunks, a, b - a, back, segs))
 
-    ncol = max(len(landpos(r, 0)), len(landpos(r, 1)))
     fill(V("uz"), 0.0)
     op("g", lambda: g.iota(T.pi[:, 0:1], [[0, 1]], 0, 1), [], [V("pi", 0, 1)])
     for t in range(2):
         e = -K - LEN[t] if plan[t][3] else 0
         op("g", lambda: g.iota(T["jt%d" % t][:, 0:6], [[64, 6]], WIN[t + 1][r][0] + e, 1, allow_small_or_imprecise_dtypes=True), [], [V("jt%d" % t, 0, 6)])
-    op("g", lambda: g.iota(T.sp[:, 0:128 * ncol], [[0, 128 * ncol]], 0, 0, allow_small_or_imprecise_dtypes=True), [], [V("sp", 0, 128 * ncol)])
-    fill(V("carry", 0, 128 * ncol), 1.0)
-    fill(V("carry", 0, 128 * ncol, 32), 0.0)
     op("v", lambda: g.vector.tensor_scalar(T.pi[:, 1:2], T.pi[:, 0:1], 96, None, Alu.bitwise_and), [V("pi", 0, 1)], [V("pi", 1, 2)])
     op("v", lambda: g.vector.tensor_scalar(T.pi[:, 2:3], T.pi[:, 0:1], 16, None, Alu.bitwise_and), [V("pi", 0, 1)], [V("pi", 2, 3)])
-    fill(V("msp"), 0.0)
     ts(V("dcol", 0, 1), V("pi", 1, 2), -0.5, None, Alu.mult)
-    fill(V("carb"), 1.0)
     tt(V("dcol", 1, 2), V("dcol", 0, 1), V("pi", 2, 3), Alu.subtract)
+    op("g", lambda: g.iota(T.ones[:], [[0, 640]], 1, 0, allow_small_or_imprecise_dtypes=True), [], [V("ones")])
+    fill(V("msp"), 0.0)
+    fill(V("carb"), 1.0)
     fill(V("carb", 0, 640, 32), 0.0)
-    fill(V("ones"), 1.0)
+    HM = 3
 
-    def tables(t, q):
+    def tables(t):
         chunks, first, n, back, segs = plan[t]
         W1, W2 = NW[t], 2 * NW[t]
-        m = len(segs)
-        h = (m + 2) // 2
 
         def put(out, c):
-            if q == "v":
-                fill(out, c)
-            else:
-                act(out, V("uz", 0, out[3] - out[2]), Act.Identity, bias=c)
+            act(out, V("uz", 0, out[3] - out[2]), Act.Identity, bias=c)
         put(V("fb%d" % t, 0, 1), float(first))
         put(V("cuh%d" % t, 0, 1), 0.0)
         put(V("cum%d" % t, 0, 1), 0.0)
         for i, (lo, hi) in enumerate(segs):
             w = hi - lo
-            c = float(lo - 1 - WIN[t][r][0] + W1 + W2 + W2 * w - (W1 * w if i < h else 0))
-            if i < h:
+            c = float(lo - 1 - WIN[t][r][0] + W1 + W2 + W2 * w - (W1 * w if i < HM else 0))
+            if i < HM:
                 put(V("ch%d" % t, 2 * HW * i + w, 2 * HW * (i + 1)), 0.0)
                 put(V("ch%d" % t, 2 * HW * i + 2 * HW - 1, 2 * HW * (i + 1)), c)
             else:
-                o = CW * (i - h)
+                o = CW * (i - HM)
                 put(V("ca%d" % t, o + w, o + CW), c if w == CW - 1 else 0.0)
                 put(V("cp%d" % t, o + w, o + CW), 0.0)
                 if w < CW - 1:
                     put(V("ca%d" % t, o + CW - 1, o + CW), c)
-        if q == "v":
-            ts(V("jt%d" % t, 6, 12), V("jt%d" % t, 0, 6), V("dcol", 1, 2), None, Alu.add)
-            ts(V("jt%d" % t, 12, 18), V("jt%d" % t, 0, 6), V("dcol", 1, 2), 1.0, Alu.add, Alu.add)
-        else:
-            act(V("jt%d" % t, 6, 12), V("jt%d" % t, 0, 6), Act.Identity, bias=V("dcol", 1, 2))
-            act(V("jt%d" % t, 12, 18), V("jt%d" % t, 6, 12), Act.Identity, bias=1.0)
+        act(V("jt%d" % t, 6, 12), V("jt%d" % t, 0, 6), Act.Identity, bias=V("dcol", 1, 2))
+        act(V("jt%d" % t, 12, 18), V("jt%d" % t, 6, 12), Act.Identity, bias=1.0)
 
-    tables(0, "s")
+    tables(0)
+    tables(1)
     for k in range(4):
         ts(V("ut", k, 512, 4), V("uz"), V("uin", k, k + 1), None, Alu.add)
     quant("u", 0, 128, V("ut"))
-    quant("r0", own0[0], own0[1], V("xt"))
+    for i in range(2):
+        quant("r0", own0[0] + 128 * i, own0[0] + 128 * i + 128, V("xt", 512 * i, 512 * i + 512))
 
     def score(t):
         q = "r%d" % t
@@ -256,15 +267,15 @@ def rank_program(g, core, T, topo):
         for i, c in enumerate(mine):
             mm(("psc", 1 + i), q, c[0] - w0, "u", 0, 128)
         lo, hi = mine[0][0] + 32 * mine[0][1], mine[-1][0] + 32 * mine[-1][2]
-        o = mm(("psc", 0), "u", 0, q, lo - w0, hi - lo)
+        mm(("psc", 0), "u", 0, q, lo - w0, hi - lo)
+        mm(("pch", 3), "u", 0, q, lo - w0, hi - lo)
         ow = V("own%d" % t, 0, n)
         copy("v", ow, V("psc", 512, 512 * n + 1, 512))
         outs = []
         for c in others:
             p = landpos(T.rank_of(c), t)[CH[t].index(mine[0])]
             outs.append(T["land%d" % t][:, p:p + n])
-        send(outs, ow, others, "arr%d" % t)
-        copy("s", V("row%d" % t, lo, hi), o)
+        send(outs, ow, others, "arr%d_%d" % (t, r))
 
     score(0)
     for s in nb:
@@ -274,37 +285,32 @@ def rank_program(g, core, T, topo):
         c, d = lo - sw[0], hi - sw[0]
         send([codes("r0c", c, d)], (codes("r0c", a, b),) + V("r0c", a, b)[1:], [T.cores[s]], "arrw")
         send([T.r0s[:, c:d]], V("r0s", a, b), [T.cores[s]], "arrw")
-    for i in range(3):
-        op("g", lambda: g.iota(T.tn0[:, NW[0] * i:NW[0] * i + NW[0]], [[4, NW[0]]], 4 * WIN[0][r][0] + (2 if i == 2 else 0), 0, allow_small_or_imprecise_dtypes=True),
-           [], [V("tn0", NW[0] * i, NW[0] * i + NW[0])])
     bank = [0]
 
     def kids(t, qs, part, cols=None):
         q, w = "r%d" % t, NW[t]
-        cols = cols or [(0, w)]
-        lo, hi = cols[0][0], cols[-1][1]
+        lo, hi = cols or (0, w)
         m0 = max(0, min(lo, hi - 128))
         n = max(hi, m0 + 128) - m0
         for i in part:
-            buf, k = ("pch", "psc")[bank[0] // 4 % 2], bank[0] % 4
+            buf, k = (("pch", 0), ("pch", 1), ("pch", 2), ("psc", 1), ("psc", 2), ("psc", 3))[bank[0] % 6]
             bank[0] += 1
             mm((buf, k), "ab"[i // 4], 128 * (i % 4), q, m0, n)
-            for x, y in cols:
-                o = V(buf, 512 * k + x - m0, 512 * k + y - m0)
-                h = V("h%s%d" % ("ab"[i // 4], t), 4 * x + i % 4, 4 * y, 4)
-                if qs[i] == "v":
-                    ts(h, o, 0.0625, None, Alu.mult)
-                else:
-                    act(h, o, Act.Copy, scale=0.0625)
+            o = V(buf, 512 * k + lo - m0, 512 * k + hi - m0)
+            h = V("h%s%d" % ("ab"[i // 4], t), 4 * lo + i % 4, 4 * hi, 4)
+            if qs[i] == "v":
+                ts(h, o, 0.0625, None, Alu.mult)
+            else:
+                act(h, o, Act.Copy, scale=0.0625)
 
-    def kidq(t, cuts, seq):
+    def kidq(t, pieces):
         q, w = "r%d" % t, NW[t]
-        cuts = [0] + cuts + [w]
-        return [lambda k=k, x=cuts[i], y=cuts[i + 1]: quant(q, (k + 1) * w + x, (k + 1) * w + y, V("h%s%d" % ("ab"[k], t), 4 * x, 4 * y)) for k, i in seq]
+        return [p and (lambda k=p[0], x=p[1], y=p[2]: quant(q, (k + 1) * w + x, (k + 1) * w + y, V("h%s%d" % ("ab"[k], t), 4 * x, 4 * y))) for p in pieces]
 
     def fillin(jobs):
-        if jobs:
-            jobs.pop(0)()
+        job = jobs.pop(0) if jobs else None
+        if job:
+            job()
 
     def spread(src, n, name):
         for b in range(4):
@@ -322,82 +328,82 @@ def rank_program(g, core, T, topo):
                 out.append((x, y, w))
         return out
 
-    def order(t, nS, flight, hook1, hook2, jobs):
+    def order(t, nS, flight1, flight2, hook2, jobs):
         chunks, first, n, back, segs = plan[t]
-        L = LEN[t]
-        W = L + 128
         lp = landpos(r, t)
-        nl = len(lp)
-        row, land = "row%d" % t, "land%d" % t
+        land, part = "land%d" % t, "part%d" % t
         mine = [k for k, c in enumerate(CH[t]) if c[3] == r]
         lo = CH[t][mine[0]][0] + 32 * CH[t][mine[0]][1]
         hi = CH[t][mine[-1]][0] + 32 * CH[t][mine[-1]][2]
-        nV = len(chunks) - nS
-        v0 = nS if r % 2 else 0
-        onS = [i for i in range(len(chunks)) if not v0 <= i < v0 + nV]
+        W = hi - lo
 
-        def val(k):
-            return V(land, lp[k], lp[k] + 1) if k in lp else V("own%d" % t, k - mine[0], k - mine[0] + 1)
+        def row(a, b):
+            return V("psc", a - lo, b - lo)
 
-        def equal(i):
-            s = CH[t][chunks[i]][0]
-            e = V("eq%d" % t, 128 * i, 128 * i + 128)
-            ts(e, V(row, s, s + 128), val(chunks[i]), None, Alu.is_equal)
-            d = V("cmp%d" % t, W * i + L, W * i + L + 128)
-            op("g", lambda: g.affine_select(d[0], e[0], [[-1, 128]], Alu.is_gt, 0.0, 0, 1), [e], [d])
+        def total_of(k, w):
+            x = CMPW * k
+            scan(V("so%d" % t, x // 2, x // 2 + w // 2), V("cmp%d" % t, x, x + w // 2), V("cmp%d" % t, x + w // 2, x + w), 0.0, Alu.add, Alu.add)
 
-        def compare(i, a, b):
-            s = CH[t][chunks[i]][0]
-            for x, y, o in ((a, min(b, s), Alu.is_ge), (max(a, s), b, Alu.is_gt)):
-                if x < y:
-                    ts(V("cmp%d" % t, W * i + x, W * i + y), V(row, x, y), val(chunks[i]), None, o)
+        def put(k, w, m):
+            z = CMPW // 2
+            copy("v", V(part, k, k + m), V("so%d" % t, z * k + w // 2 - 1, z * (k + m - 1) + w // 2, z) if m > 1 else V("so%d" % t, z * k + w // 2 - 1, z * k + w // 2))
 
-        def count_of(i):
-            scan(V("so%d" % t, W // 2 * i, W // 2 * i + W // 2), V("cmp%d" % t, W * i, W * i + W // 2), V("cmp%d" % t, W * i + W // 2, W * i + W), 0.0, Alu.add, Alu.add)
-
-        early = [i for i in range(v0, v0 + nV) if chunks[i] in mine and lo <= CH[t][chunks[i]][0] and CH[t][chunks[i]][0] + 128 <= hi]
-        for i in early:
-            equal(i)
-            compare(i, lo, hi)
-        flight()
-        spread(land, nl, "sp")
-        scan(V("rep", 0, 128 * nl), V("carry", 0, 128 * nl), V("sp", 0, 128 * nl), 0.0, Alu.mult, Alu.add)
-        for i, x in enumerate(onS):
-            act(V("neg%d" % t, i, i + 1), val(chunks[x]), Act.Copy, scale=-1.0)
-        for x, y, w in runs([CH[t][k] for k in sorted(lp, key=lambda k: lp[k])], 0, L):
-            turn(V(row, y, y + w), V("rep", x, x + w))
-        hook1()
-        for i in range(len(chunks)):
-            if i not in early:
-                equal(i)
-        for i, c in enumerate(onS):
-            s = CH[t][chunks[c]][0]
-            o = 1088 * i
-            act(V("sg%d" % t, o, o + L), V(row, 0, L), Act.Sign, bias=V("neg%d" % t, i, i + 1))
-            if s:
-                act(V("sj%d" % t, o, o + s), V("sg%d" % t, o, o + s), Act.Relu, scale=-1.0, accum=V("acc%d" % t, 2 * i, 2 * i + 1))
-            act(V("sj%d" % t, o + s, o + L), V("sg%d" % t, o + s, o + L), Act.Relu, accum=V("acc%d" % t, 2 * i + 1, 2 * i + 2))
-        for i in range(v0, v0 + nV):
-            if i in early:
-                compare(i, 0, lo)
-                compare(i, hi, L)
-            else:
-                compare(i, 0, L)
-            if i > v0:
-                count_of(i - 1)
-        for i, c in enumerate(onS):
-            d = V("cmp%d" % t, W * c + L, W * c + L + 128)
-            tr = V("tri%d" % t, i, i + 1)
-            op("v", lambda: g.vector.tensor_reduce(tr[0], d[0], AxisListType.X, Alu.add), [d], [tr])
-        count_of(v0 + nV - 1)
-        for i, c in enumerate(onS):
-            if CH[t][chunks[c]][0]:
-                ts(V("rho%d" % t, i, i + 1), V("acc%d" % t, 2 * i + 1, 2 * i + 2), V("acc%d" % t, 2 * i, 2 * i + 1), V("tri%d" % t, i, i + 1), Alu.subtract, Alu.add)
-            else:
-                tt(V("rho%d" % t, i, i + 1), V("acc%d" % t, 2 * i + 1, 2 * i + 2), V("tri%d" % t, i, i + 1), Alu.add)
-        ts(V("mk%d" % t, v0, v0 + nV), V("so%d" % t, W // 2 * v0 + W // 2 - 1, W // 2 * (v0 + nV), W // 2), float(K), None, Alu.is_lt)
-        for i, c in enumerate(onS):
-            ts(V("mk%d" % t, c, c + 1), V("rho%d" % t, i, i + 1), float(K - CH[t][chunks[c]][0]), None, Alu.is_lt)
+        wide = {}
+        for i, k in enumerate(mine):
+            s = CH[t][k][0]
+            e = min(s + 128, hi)
+            val = V("own%d" % t, i, i + 1)
+            x = CMPW * k
+            q = V("eq%d" % t, 128 * i, 128 * i + e - s)
+            d = V("cmp%d" % t, x + W, x + W + e - s)
+            ts(q, row(s, e), val, None, Alu.is_equal)
+            op("g", lambda: g.affine_select(d[0], q[0], [[-1, e - s]], Alu.is_gt, 0.0, 0, 1), [q], [d])
+            if s > lo:
+                ts(V("cmp%d" % t, x, x + s - lo), row(lo, s), val, None, Alu.is_ge)
+            ts(V("cmp%d" % t, x + s - lo, x + W), row(s, hi), val, None, Alu.is_gt)
+            wide[k] = W + e - s
+        flight1()
+        turns = sorted(others_r, key=lambda s: (not topo.same_plane(topo.chip(core), topo.chip(T.cores[s])), s))
+        onS = turns[len(turns) - nS:]
+        i = 0
+        for s in onS:
+            for k in [k for k, c in enumerate(CH[t]) if c[3] == s]:
+                act(V("sg%d" % t, 320 * i, 320 * i + W), V("pch", 1536, 1536 + W), Act.Sign, bias=V(land, lp[k], lp[k] + 1), scale=-1.0)
+                act(V("sj%d" % t, 320 * i, 320 * i + W), V("sg%d" % t, 320 * i, 320 * i + W), Act.Relu, scale=1.0 if r < s else -1.0, accum=V("acc%d" % t, i, i + 1))
+                act(V(part, k, k + 1), V("acc%d" % t, i, i + 1), Act.Copy, scale=-1.0 if r < s else 1.0, bias=float(W) if r < s else 0.0)
+                i += 1
+        last = None
+        for s in turns[:len(turns) - nS]:
+            ks = [k for k, c in enumerate(CH[t]) if c[3] == s]
+            for k in ks:
+                ts(V("cmp%d" % t, CMPW * k, CMPW * k + W), row(lo, hi), V(land, lp[k], lp[k] + 1), None, Alu.is_ge if r < s else Alu.is_gt)
+                if last is not None:
+                    total_of(last, W)
+                last = k
+        total_of(last, W)
+        for k in mine:
+            total_of(k, wide[k])
+        put(mine[0], wide[mine[0]], 2)
+        for k in mine[2:]:
+            put(k, wide[k], 1)
+        for s in turns[:len(turns) - nS]:
+            ks = [k for k, c in enumerate(CH[t]) if c[3] == s]
+            put(ks[0], W, len(ks))
+        jb = []
+        for h in half:
+            cs = [c for c in h if c != core]
+            k0 = group(T.rank_of(h[0]), t)[0]
+            jb.append(([T["pland%d" % t][:, 5 * slot(T.rank_of(c), r):5 * slot(T.rank_of(c), r) + 5] for c in cs], V(part, k0, k0 + 5), cs))
+        send_halves(jb, "cnt%d_%d" % (t, r))
+        flight2()
+        k0, m = chunks[0], len(chunks)
+        o = chunks[0] - group(r, t)[0]
+        land_of = [V("pland%d" % t, 5 * slot(r, s) + o, 5 * slot(r, s) + o + m) for s in turns]
+        sums = [V("rho%d" % t, 5 * i, 5 * i + m) for i in range(3)]
+        tt(sums[0], V(part, k0, k0 + m), land_of[0], Alu.add)
+        tt(sums[1], land_of[1], land_of[2], Alu.add)
+        tt(sums[2], sums[0], sums[1], Alu.add)
+        ts(V("mk%d" % t, 0, m), sums[2], float(K), None, Alu.is_lt)
         spread("mk%d" % t, len(chunks), "msp")
         hook2()
         fillin(jobs)
@@ -413,7 +419,7 @@ def rank_program(g, core, T, topo):
         fillin(jobs)
         W1, W2 = NW[t], 2 * NW[t]
         m = len(segs)
-        hm = (m + 2) // 2
+        hm = HM
         z = m - hm
         jj = "jt%d" % t
         if back:
@@ -462,39 +468,46 @@ def rank_program(g, core, T, topo):
 
     border = [(0, own0[0])] * (own0[0] > 0) + [(own0[1], NW[0])] * (own0[1] < NW[0])
 
-    def own_first_kids():
+    def flight_of_scores0():
         quant("a", 0, 512, V("at"))
-        kids(0, "ssssssss", range(4), [own0])
+
+    def flight_of_counts0():
+        kids(0, "ssssssss", range(4), own0)
         quant("b", 0, 512, V("bt"))
+        kids(0, "ssssssss", range(4, 5))
+        for i in range(3):
+            op("g", lambda: g.iota(T.tn0[:, NW[0] * i:NW[0] * i + NW[0]], [[4, NW[0]]], 4 * WIN[0][r][0] + (2 if i == 2 else 0), 0, allow_small_or_imprecise_dtypes=True),
+               [], [V("tn0", NW[0] * i, NW[0] * i + NW[0])])
 
-    def own_second_kids():
-        kids(0, "ssssssss", range(4, 8), [own0])
-
-    def border_kids():
-        kids(0, "ssssssss", range(8), border)
+    def rest_kids():
+        kids(0, "ssssssss", range(5, 8))
+        for x in border:
+            kids(0, "ssssssss", range(4), x)
     if len(border) == 2:
-        jobs = kidq(0, [144, 288], [(0, 1), (1, 1), (0, 0), (0, 2), (1, 0), (1, 2)])
+        jobs = [(0, 144, 288), None, None, None, (1, 0, NW[0]), (0, 0, 144), (0, 288, NW[0])]
+    elif r == 0:
+        jobs = [(0, 0, 144), None, None, None, (1, 0, NW[0]), (0, 144, NW[0])]
     else:
-        own, edge = (0, 1) if r == 0 else (1, 0)
-        jobs = kidq(0, [144], [(0, own), (1, own), (0, edge), (1, edge)])
-    order(0, 2 if len(plan[0][0]) > 3 else 1, own_first_kids, own_second_kids, border_kids, jobs)
+        jobs = [(0, 144, NW[0]), None, None, None, (1, 0, NW[0]), (0, 0, 144)]
+    order(0, 1, flight_of_scores0, flight_of_counts0, rest_kids, kidq(0, jobs))
     pick(0)
     score(1)
+    bank[0] = 0
 
-    def first_kids():
-        kids(1, "vsvsssss", range(4))
-        tables(1, "v")
+    def flight_of_scores1():
+        kids(1, "sss", range(3))
+
+    def flight_of_counts1():
+        kids(1, "sssvvvss", range(3, 8))
         quant("w", 0, 128, V("wt"))
-        kidq(1, [], [(0, 0)])[0]()
-
-    def second_kids():
-        kids(1, "vsvsssss", range(4, 8))
+        for job in kidq(1, [(0, 0, NW[1]), (1, 0, NW[1])]):
+            job()
 
     def new_numbers():
         numbers(0, V("tn1", 0, NW[1]))
         copy("s", V("tn1", NW[1], 2 * NW[1]), V("tn1", 0, NW[1]))
         act(V("tn1", 2 * NW[1], 3 * NW[1]), V("tn1", 0, NW[1]), Act.Identity, bias=1.0)
-    order(1, 2 if len(plan[1][0]) > 3 else 1, first_kids, second_kids, new_numbers, kidq(1, [176 if NW[1] > 300 else 144], [(1, 0), (1, 1)]))
+    order(1, 1, flight_of_scores1, flight_of_counts1, new_numbers, [])
     cut = ((0, 160), (160, E))
     for x, y in cut:
         pick(1, x, y)
@@ -503,15 +516,16 @@ def rank_program(g, core, T, topo):
 
     def scales(q, k):
         dma(q, T.osc[4 * k:4 * k + 4, :], T.r2s[32 * k:32 * k + 4, :], "out", [V("r2s")], [])
-    dma("y", T.oc[:], codes("r2c", 0, E), "out", [V("r2c")], [])
+    for x, y in cut:
+        dma("y", T.oc[:, 4 * x:4 * y], codes("r2c", x, y), "out", [V("r2c", x, y)], [])
     scales("y", 0)
     scales("y", 1)
-    dma("s", T.hs[:], T.hsr[0:1, :], "out", [V("hsr")], [])
     scales("s", 2)
     scales("s", 3)
+    dma("s", T.hs[:], T.hsr[0:1, :], "out", [V("hsr")], [])
     for o, (x, y) in zip(outs, cut):
         copy("v", V("ysb", x, y), o)
-    dma("y", T.y[:], T.ysb[:], "out", [V("ysb")], [])
+        dma("y", T.y[:, x:y], T.ysb[:, x:y], "out", [V("ysb", x, y)], [])
     for s in sorted(total):
         if known["g"].get(s, 0) < total[s]:
             g.wait_ge(T.sem[s], total[s])

@@ -8,14 +8,16 @@ CH = ([(128 * c, 0, 4, c // 2) for c in range(8)],
 WIN = ([(0, 288), (160, 576), (448, 864), (736, 1024)], [(0, 288), (224, 576), (512, 864), (800, 1088)], [(E * r, E * r + E) for r in range(N)])
 NEED = ([(0, 288), (0, 576), (448, 1024), (736, 1024)], [(0, 288), (0, 576), (512, 1088), (800, 1088)])
 F32, BF, I32, U16 = "float32", "bfloat16", "int32", "uint16"
-CW = 131
-HW = 66
+SW = 130
+CW = 132
+PAD = 64
+NV = (6, 3)
 CMPW = 448
 
 SCRATCH = {
     "xt": ("sbuf", [128, 1024], BF), "uin": ("sbuf", [128, 8], BF), "ut": ("sbuf", [128, 512], BF), "uz": ("sbuf", [128, 128], BF),
     "at": ("sbuf", [128, 2048], BF), "bt": ("sbuf", [128, 2048], BF), "wt": ("sbuf", [128, 512], BF),
-    "msp": ("sbuf", [128, 640], BF), "mrep": ("sbuf", [128, 640], BF), "ones": ("sbuf", [128, 640], BF), "carb": ("sbuf", [128, 640], BF),
+    "msp": ("sbuf", [128, 640], BF), "mrep": ("sbuf", [128, 640], BF), "carb": ("sbuf", [128, 640], BF),
     "pi": ("sbuf", [128, 4], I32), "dcol": ("sbuf", [128, 2], F32),
     "psc": ("psum", [128, 2048], F32), "pch": ("psum", [128, 2048], F32),
     "ysb": ("sbuf", [128, 288], F32), "hsr": ("sbuf", [128, 288], F32),
@@ -27,10 +29,9 @@ for _q, _n in (("u", 128), ("a", 512), ("b", 512), ("w", 128), ("r0", 1248), ("r
 for _t in range(2):
     for _n, _w, _d in (("ha", 1664, BF), ("hb", 1664, BF), ("own", 4, F32), ("land", 8, F32), ("cmp", 9 * CMPW, BF),
                        ("eq", 384, BF), ("sg", 3 * 320, BF), ("sj", 3 * 320, BF), ("so", 9 * CMPW // 2, BF), ("acc", 3, F32),
-                       ("part", 9, BF), ("pland", 16, BF), ("rho", 15, F32), ("mk", 5, F32), ("mrow", 640, BF), ("fb", 644, F32),
-                       ("ch", 12 * HW, F32), ("ca", 3 * CW, F32), ("cp", 3 * CW, F32),
-                       ("cuh", 6 * HW + 4, F32), ("cum", 3 * CW + 4, F32), ("jt", 18, F32), ("jj", 18, F32), ("fs", 12 * CW, BF), ("sa", 6, F32), ("sb", 6, F32),
-                       ("xa", 6, F32), ("xb", 6, F32), ("dd", 6, F32), ("ll", 6, F32), ("wf", 24, F32), ("wu", 24, U16)):
+                       ("pland", 16, BF), ("rho", 15, F32), ("mrow", 640, BF), ("inc", 704, BF), ("fb", 752, BF),
+                       ("jt", 18, F32), ("jj", 12, F32), ("xc", 1, F32), ("ch", 6 * CW, BF), ("fs", 6 * CW, BF), ("cu", 1 + 6 * CW // 2, F32),
+                       ("sm", 6, F32), ("qi", 6, I32), ("ws", 6, F32), ("wy", 6, F32), ("ll", 6, F32), ("wf", 24, F32), ("wu", 24, U16)):
         SCRATCH["%s%d" % (_n, _t)] = ("sbuf", [128, _w], _d)
 SEMAPHORES = ["v", "s", "p", "gc", "sent", "arrw", "dx0", "dx1", "du", "da", "db", "dw", "out"] + ["%s%d_%d" % (k, t, r) for k in ("arr", "cnt") for t in range(2) for r in range(N)]
 
@@ -150,14 +151,6 @@ def rank_program(g, core, T, topo):
                                               srcs=[src[0]], dsts=outs)], local_sem=T.sem.sent)
         total["sent"] = total.get("sent", 0) + len(e)
 
-    def send_halves(jobs, sem):
-        e = engines(others)
-        h = len(e) // 2
-        need("g", [j[1] for j in jobs], [])
-        g.remote_dma_fused([RemoteDMATransfer(dst_ids=[dst(c) for c in cs], dma_engine_mask=sum(1 << k for k in e[h * i:h * i + h]), remote_sem=T.sem[sem],
-                                              srcs=[src[0]], dsts=outs) for i, (outs, src, cs) in enumerate(jobs)], local_sem=T.sem.sent)
-        total["sent"] = total.get("sent", 0) + 2 * h
-
     def arrive(sem, n, views):
         total[sem] = total.get(sem, 0) + n
         for v in views:
@@ -166,8 +159,16 @@ def rank_program(g, core, T, topo):
     def codes(name, a, b):
         return T[name][:, a:b].bitcast(dt.uint8)
 
+    def near(c, d):
+        return topo.same_plane(topo.chip(c), topo.chip(d))
+
+    def targets(c):
+        i = T.rank_of(c)
+        return sorted([d for d in T.cores if d != c], key=lambda d: (near(c, d), (T.rank_of(d) - i) % N))
+
     NW = [WIN[t][r][1] - WIN[t][r][0] for t in range(3)]
-    others = [c for c in T.cores if c != core]
+    C = (NW[0], NW[1], 0)
+    others = targets(core)
     others_r = [T.rank_of(c) for c in others]
     ENG = len(engines(others))
     half = (T.cores[:N // 2], T.cores[N // 2:])
@@ -193,75 +194,104 @@ def rank_program(g, core, T, topo):
     wviews = []
     for s in nb:
         a, b = (0, own0[0]) if s < r else (own0[1], NW[0])
-        wviews += [V("r0c", a, b), V("r0s", a, b)]
+        wviews += [V("r0c", C[0] + a, C[0] + b), V("r0s", C[0] + a, C[0] + b)]
     arrive("arrw", 2 * ENG * len(nb), wviews)
     for t in range(2):
         for s in others_r:
             cols = [landpos(r, t)[k] for k, c in enumerate(CH[t]) if c[3] == s]
             arrive("arr%d_%d" % (t, s), ENG, [V("land%d" % t, cols[0], cols[-1] + 1)])
-            arrive("cnt%d_%d" % (t, s), ENG // 2, [V("pland%d" % t, 5 * slot(r, s), 5 * slot(r, s) + 5)])
+            arrive("cnt%d_%d" % (t, s), ENG, [V("pland%d" % t, 5 * slot(r, s), 5 * slot(r, s) + 5)])
 
     plan = []
     for t in range(2):
         a, b = NEED[t][r]
         chunks = [k for k, c in enumerate(CH[t]) if c[0] + 32 * c[2] > a and c[0] + 32 * c[1] < b]
         back = a > 0
-        segs = []
-        for i in range((NW[t + 1] + 63) // 64):
-            j0 = WIN[t + 1][r][0] + 64 * i
-            segs.append((max(j0 - 64, a), min(j0 + 66, b + 1)))
-        plan.append((chunks, a, b - a, back, segs))
+        end = WIN[t][r][1]
+        lo1, hi1 = WIN[t + 1][r]
+        mid = (lo1 + end) // 2 if back else (lo1 + hi1) // 2
+        plan.append((chunks, a, b - a, back, end, mid, (hi1 - lo1 + 63) // 64))
+
+    def runs(chs, base, size):
+        out = []
+        for i, c in enumerate(chs):
+            lo, hi = max(c[0] + 32 * c[1], base), min(c[0] + 32 * c[2], base + size)
+            x, y, w = 128 * i + lo - c[0], lo - base, hi - lo
+            if out and out[-1][0] + out[-1][2] == x and out[-1][1] + out[-1][2] == y:
+                out[-1] = (out[-1][0], out[-1][1], out[-1][2] + w)
+            else:
+                out.append((x, y, w))
+        return out
+
+    def slice_of(t, i):
+        c = WIN[t + 1][r][0] + 64 * i - 64 - plan[t][1] + PAD
+        return c, c + SW
 
     fill(V("uz"), 0.0)
     op("g", lambda: g.iota(T.pi[:, 0:1], [[0, 1]], 0, 1), [], [V("pi", 0, 1)])
     for t in range(2):
-        e = -K - LEN[t] if plan[t][3] else 0
+        e = -1 - K - plan[t][4] if plan[t][3] else -1 - plan[t][5]
         op("g", lambda: g.iota(T["jt%d" % t][:, 0:6], [[64, 6]], WIN[t + 1][r][0] + e, 1, allow_small_or_imprecise_dtypes=True), [], [V("jt%d" % t, 0, 6)])
     op("v", lambda: g.vector.tensor_scalar(T.pi[:, 1:2], T.pi[:, 0:1], 96, None, Alu.bitwise_and), [V("pi", 0, 1)], [V("pi", 1, 2)])
     op("v", lambda: g.vector.tensor_scalar(T.pi[:, 2:3], T.pi[:, 0:1], 16, None, Alu.bitwise_and), [V("pi", 0, 1)], [V("pi", 2, 3)])
-    ts(V("dcol", 0, 1), V("pi", 1, 2), -0.5, None, Alu.mult)
-    tt(V("dcol", 1, 2), V("dcol", 0, 1), V("pi", 2, 3), Alu.subtract)
-    op("g", lambda: g.iota(T.ones[:], [[0, 640]], 1, 0, allow_small_or_imprecise_dtypes=True), [], [V("ones")])
+    ts(V("dcol", 0, 1), V("pi", 1, 2), -1.0, None, Alu.mult)
+    ts(V("dcol", 1, 2), V("pi", 2, 3), -2.0, V("dcol", 0, 1), Alu.mult, Alu.add)
     fill(V("msp"), 0.0)
     fill(V("carb"), 1.0)
     fill(V("carb", 0, 640, 32), 0.0)
-    HM = 3
+
+    def steps(t):
+        chunks, first, n, back, end, mid, m = plan[t]
+        for x, y, w in runs([CH[t][k] for k in chunks], first, n):
+            odd = x // 32 % 2
+            n2 = (w + 63) // 64
+            op("g", lambda: g.iota(T["inc%d" % t][:, y:y + 64 * n2], [[0, n2], [1 - 2 * odd, 2], [0, 32]], 2 + odd, 0, allow_small_or_imprecise_dtypes=True),
+               [], [V("inc%d" % t, y, y + 64 * n2)])
+
+    def last_steps(t):
+        chunks, first, n, back, end, mid, m = plan[t]
+        x, y, w = runs([CH[t][k] for k in chunks], first, n)[-1]
+        last = 2 + (x + w - 32) // 32 % 2
+        far = 2 * (first + n - end)
+        if far:
+            fill(V("inc%d" % t, n - 1, n), float(last - 256))
+            fill(V("inc%d" % t, n - 2, n - 1), float(last - (far - 256)))
 
     def tables(t):
-        chunks, first, n, back, segs = plan[t]
-        W1, W2 = NW[t], 2 * NW[t]
+        chunks, first, n, back, end, mid, m = plan[t]
+        fb, lo1 = "fb%d" % t, WIN[t + 1][r][0]
 
         def put(out, c):
-            act(out, V("uz", 0, out[3] - out[2]), Act.Identity, bias=c)
-        put(V("fb%d" % t, 0, 1), float(first))
-        put(V("cuh%d" % t, 0, 1), 0.0)
-        put(V("cum%d" % t, 0, 1), 0.0)
-        for i, (lo, hi) in enumerate(segs):
-            w = hi - lo
-            c = float(lo - 1 - WIN[t][r][0] + W1 + W2 + W2 * w - (W1 * w if i < HM else 0))
-            if i < HM:
-                put(V("ch%d" % t, 2 * HW * i + w, 2 * HW * (i + 1)), 0.0)
-                put(V("ch%d" % t, 2 * HW * i + 2 * HW - 1, 2 * HW * (i + 1)), c)
-            else:
-                o = CW * (i - HM)
-                put(V("ca%d" % t, o + w, o + CW), c if w == CW - 1 else 0.0)
-                put(V("cp%d" % t, o + w, o + CW), 0.0)
-                if w < CW - 1:
-                    put(V("ca%d" % t, o + CW - 1, o + CW), c)
-        act(V("jt%d" % t, 6, 12), V("jt%d" % t, 0, 6), Act.Identity, bias=V("dcol", 1, 2))
-        act(V("jt%d" % t, 12, 18), V("jt%d" % t, 6, 12), Act.Identity, bias=1.0)
+            act(out, V("uz", 0, out[3] - out[2]), Act.Identity, bias=float(c))
+        put(V(fb, PAD, PAD + 1), 2 * (first - mid))
+        if slice_of(t, 0)[0] < PAD:
+            put(V(fb, 0, PAD), -600)
+        z = slice_of(t, m - 1)[1]
+        if z > PAD + n + 1:
+            put(V(fb, PAD + n + 1, z), 600)
+        put(V("cu%d" % t, 0, 1), 0)
+        for i in range(m):
+            k = -(i * (128 * SW + 384) + 6 * (lo1 - 64 - WIN[t][r][0]) - 6)
+            hi = (k // 512) * 512
+            put(V("ch%d" % t, CW * i + SW, CW * i + SW + 1), hi)
+            put(V("ch%d" % t, CW * i + SW + 1, CW * i + CW), k - hi)
+        act(V("jt%d" % t, 6, 12), V("jt%d" % t, 0, 6), Act.Identity, bias=V("dcol", 1, 2), scale=2.0)
+        act(V("jt%d" % t, 12, 18), V("jt%d" % t, 6, 12), Act.Identity, bias=6.0)
+        if not back:
+            act(V("xc%d" % t), V("jt%d" % t, 12, 13), Act.Copy, scale=float(SW))
 
+    steps(0)
     tables(0)
     tables(1)
     for k in range(4):
         ts(V("ut", k, 512, 4), V("uz"), V("uin", k, k + 1), None, Alu.add)
     quant("u", 0, 128, V("ut"))
     for i in range(2):
-        quant("r0", own0[0] + 128 * i, own0[0] + 128 * i + 128, V("xt", 512 * i, 512 * i + 512))
+        quant("r0", C[0] + own0[0] + 128 * i, C[0] + own0[0] + 128 * i + 128, V("xt", 512 * i, 512 * i + 512))
 
     def score(t):
         q = "r%d" % t
-        w0 = WIN[t][r][0]
+        w0 = WIN[t][r][0] - C[t]
         mine = [c for c in CH[t] if c[3] == r]
         n = len(mine)
         for i, c in enumerate(mine):
@@ -281,8 +311,9 @@ def rank_program(g, core, T, topo):
     for s in nb:
         sw = WIN[0][s]
         lo, hi = max(P * r, sw[0]), min(P * r + P, sw[1])
-        a, b = lo - WIN[0][r][0], hi - WIN[0][r][0]
-        c, d = lo - sw[0], hi - sw[0]
+        a, b = lo - WIN[0][r][0] + C[0], hi - WIN[0][r][0] + C[0]
+        e = sw[1] - sw[0] - sw[0]
+        c, d = lo + e, hi + e
         send([codes("r0c", c, d)], (codes("r0c", a, b),) + V("r0c", a, b)[1:], [T.cores[s]], "arrw")
         send([T.r0s[:, c:d]], V("r0s", a, b), [T.cores[s]], "arrw")
     bank = [0]
@@ -295,7 +326,7 @@ def rank_program(g, core, T, topo):
         for i in part:
             buf, k = (("pch", 0), ("pch", 1), ("pch", 2), ("psc", 1), ("psc", 2), ("psc", 3))[bank[0] % 6]
             bank[0] += 1
-            mm((buf, k), "ab"[i // 4], 128 * (i % 4), q, m0, n)
+            mm((buf, k), "ab"[i // 4], 128 * (i % 4), q, C[t] + m0, n)
             o = V(buf, 512 * k + lo - m0, 512 * k + hi - m0)
             h = V("h%s%d" % ("ab"[i // 4], t), 4 * lo + i % 4, 4 * hi, 4)
             if qs[i] == "v":
@@ -305,34 +336,19 @@ def rank_program(g, core, T, topo):
 
     def kidq(t, pieces):
         q, w = "r%d" % t, NW[t]
-        return [p and (lambda k=p[0], x=p[1], y=p[2]: quant(q, (k + 1) * w + x, (k + 1) * w + y, V("h%s%d" % ("ab"[k], t), 4 * x, 4 * y))) for p in pieces]
+        return [p and (lambda k=p[0], x=p[1], y=p[2]: quant(q, 2 * k * w + x, 2 * k * w + y, V("h%s%d" % ("ab"[k], t), 4 * x, 4 * y))) for p in pieces]
 
     def fillin(jobs):
         job = jobs.pop(0) if jobs else None
         if job:
             job()
 
-    def spread(src, n, name):
-        for b in range(4):
-            for a in range(4):
-                copy("vs"[(a + b) % 2], V(name, 32 * a, 128 * n, 128, 32 * b, 32 * b + 32), V(src, 0, n, 1, 32 * a, 32 * a + 32))
-
-    def runs(chs, base, size):
-        out = []
-        for i, c in enumerate(chs):
-            lo, hi = max(c[0] + 32 * c[1], base), min(c[0] + 32 * c[2], base + size)
-            x, y, w = 128 * i + lo - c[0], lo - base, hi - lo
-            if out and out[-1][0] + out[-1][2] == x and out[-1][1] + out[-1][2] == y:
-                out[-1] = (out[-1][0], out[-1][1], out[-1][2] + w)
-            else:
-                out.append((x, y, w))
-        return out
-
-    def order(t, nS, flight1, flight2, hook2, jobs):
-        chunks, first, n, back, segs = plan[t]
+    def order(t, flight1, flight2, hook2, jobs):
+        chunks, first, n, back, end, mid, m = plan[t]
         lp = landpos(r, t)
-        land, part = "land%d" % t, "part%d" % t
-        mine = [k for k, c in enumerate(CH[t]) if c[3] == r]
+        land, so, z = "land%d" % t, "so%d" % t, CMPW // 2
+        chunks_of = [[k for k, c in enumerate(CH[t]) if c[3] == s] for s in range(N)]
+        mine = chunks_of[r]
         lo = CH[t][mine[0]][0] + 32 * CH[t][mine[0]][1]
         hi = CH[t][mine[-1]][0] + 32 * CH[t][mine[-1]][2]
         W = hi - lo
@@ -341,12 +357,11 @@ def rank_program(g, core, T, topo):
             return V("psc", a - lo, b - lo)
 
         def total_of(k, w):
-            x = CMPW * k
-            scan(V("so%d" % t, x // 2, x // 2 + w // 2), V("cmp%d" % t, x, x + w // 2), V("cmp%d" % t, x + w // 2, x + w), 0.0, Alu.add, Alu.add)
+            x, y = CMPW * k, w // 2
+            scan(V(so, 9 * (z - y) + k, 9 * (z - 1) + k + 1, 9), V("cmp%d" % t, x, x + y), V("cmp%d" % t, x + y, x + w), 0.0, Alu.add, Alu.add)
 
-        def put(k, w, m):
-            z = CMPW // 2
-            copy("v", V(part, k, k + m), V("so%d" % t, z * k + w // 2 - 1, z * (k + m - 1) + w // 2, z) if m > 1 else V("so%d" % t, z * k + w // 2 - 1, z * k + w // 2))
+        def part(k, m=1):
+            return V(so, 9 * (z - 1) + k, 9 * (z - 1) + k + m, 9 if m == 1 else 1)
 
         wide = {}
         for i, k in enumerate(mine):
@@ -363,19 +378,15 @@ def rank_program(g, core, T, topo):
             ts(V("cmp%d" % t, x + s - lo, x + W), row(s, hi), val, None, Alu.is_gt)
             wide[k] = W + e - s
         flight1()
-        turns = sorted(others_r, key=lambda s: (not topo.same_plane(topo.chip(core), topo.chip(T.cores[s])), s))
-        onS = turns[len(turns) - nS:]
-        i = 0
-        for s in onS:
-            for k in [k for k, c in enumerate(CH[t]) if c[3] == s]:
-                act(V("sg%d" % t, 320 * i, 320 * i + W), V("pch", 1536, 1536 + W), Act.Sign, bias=V(land, lp[k], lp[k] + 1), scale=-1.0)
-                act(V("sj%d" % t, 320 * i, 320 * i + W), V("sg%d" % t, 320 * i, 320 * i + W), Act.Relu, scale=1.0 if r < s else -1.0, accum=V("acc%d" % t, i, i + 1))
-                act(V(part, k, k + 1), V("acc%d" % t, i, i + 1), Act.Copy, scale=-1.0 if r < s else 1.0, bias=float(W) if r < s else 0.0)
-                i += 1
+        first_r, second_r, third_r = sorted(others_r, key=lambda s: targets(T.cores[s]).index(core))
+        byS, byV = (third_r, second_r) if len(chunks_of[second_r]) > len(chunks_of[third_r]) else (second_r, third_r)
+        for i, k in enumerate(chunks_of[byS]):
+            act(V("sg%d" % t, 320 * i, 320 * i + W), V("pch", 1536, 1536 + W), Act.Sign, bias=V(land, lp[k], lp[k] + 1), scale=-1.0)
+            act(V("sj%d" % t, 320 * i, 320 * i + W), V("sg%d" % t, 320 * i, 320 * i + W), Act.Relu, scale=1.0 if r < byS else -1.0, accum=V("acc%d" % t, i, i + 1))
+            act(part(k), V("acc%d" % t, i, i + 1), Act.Copy, scale=-1.0 if r < byS else 1.0, bias=float(W) if r < byS else 0.0)
         last = None
-        for s in turns[:len(turns) - nS]:
-            ks = [k for k, c in enumerate(CH[t]) if c[3] == s]
-            for k in ks:
+        for s in (first_r, byV):
+            for k in chunks_of[s]:
                 ts(V("cmp%d" % t, CMPW * k, CMPW * k + W), row(lo, hi), V(land, lp[k], lp[k] + 1), None, Alu.is_ge if r < s else Alu.is_gt)
                 if last is not None:
                     total_of(last, W)
@@ -383,28 +394,26 @@ def rank_program(g, core, T, topo):
         total_of(last, W)
         for k in mine:
             total_of(k, wide[k])
-        put(mine[0], wide[mine[0]], 2)
-        for k in mine[2:]:
-            put(k, wide[k], 1)
-        for s in turns[:len(turns) - nS]:
-            ks = [k for k, c in enumerate(CH[t]) if c[3] == s]
-            put(ks[0], W, len(ks))
-        jb = []
-        for h in half:
-            cs = [c for c in h if c != core]
+        for h in sorted(half, key=lambda h: core not in h):
+            cs = [c for c in others if c in h]
             k0 = group(T.rank_of(h[0]), t)[0]
-            jb.append(([T["pland%d" % t][:, 5 * slot(T.rank_of(c), r):5 * slot(T.rank_of(c), r) + 5] for c in cs], V(part, k0, k0 + 5), cs))
-        send_halves(jb, "cnt%d_%d" % (t, r))
+            send([T["pland%d" % t][:, 5 * slot(T.rank_of(c), r):5 * slot(T.rank_of(c), r) + 5] for c in cs], part(k0, 5), cs, "cnt%d_%d" % (t, r))
         flight2()
-        k0, m = chunks[0], len(chunks)
+        k0, nc = chunks[0], len(chunks)
         o = chunks[0] - group(r, t)[0]
-        land_of = [V("pland%d" % t, 5 * slot(r, s) + o, 5 * slot(r, s) + o + m) for s in turns]
-        sums = [V("rho%d" % t, 5 * i, 5 * i + m) for i in range(3)]
-        tt(sums[0], V(part, k0, k0 + m), land_of[0], Alu.add)
-        tt(sums[1], land_of[1], land_of[2], Alu.add)
-        tt(sums[2], sums[0], sums[1], Alu.add)
-        ts(V("mk%d" % t, 0, m), sums[2], float(K), None, Alu.is_lt)
-        spread("mk%d" % t, len(chunks), "msp")
+        at = part(k0, nc)
+        for i, s in enumerate(sorted(others_r, key=lambda s: (s // 2 != r // 2, near(core, T.cores[s])))):
+            to = V("rho%d" % t, 5 * i, 5 * i + nc)
+            tt(to, at, V("pland%d" % t, 5 * slot(r, s) + o, 5 * slot(r, s) + o + nc), Alu.add)
+            at = to
+        for b in range(4):
+            for a in range(4):
+                src = V("rho%d" % t, 10, 10 + nc, 1, 32 * a, 32 * a + 32)
+                to = V("msp", 32 * a, 128 * nc, 128, 32 * b, 32 * b + 32)
+                if a % 2:
+                    act(to, src, Act.Sign, bias=K - 0.5, scale=-1.0)
+                else:
+                    ts(to, src, float(K), 2.0, Alu.is_lt, Alu.mult)
         hook2()
         fillin(jobs)
         pieces = runs([CH[t][k] for k in chunks], first, n)
@@ -415,40 +424,35 @@ def rank_program(g, core, T, topo):
             turn(V("mrow%d" % t, y, y + w), V("mrep", x, x + w))
         fillin(jobs)
         fb = "fb%d" % t
-        scan(V(fb, 1, n + 1), V("mrow%d" % t, 0, n), V("ones", 0, n), float(first), Alu.add, Alu.add)
+        scan(V(fb, PAD + 1, PAD + n + 1), V("mrow%d" % t, 0, n), V("inc%d" % t, 0, n), float(2 * (first - mid)), Alu.add, Alu.add)
         fillin(jobs)
-        W1, W2 = NW[t], 2 * NW[t]
-        m = len(segs)
-        hm = HM
-        z = m - hm
-        jj = "jt%d" % t
+        jj, o = "jt%d" % t, 6
         if back:
-            jj = "jj%d" % t
-            ts(V(jj, 6, 18), V("jt%d" % t, 6, 18), V(fb, n, n + 1), None, Alu.add)
-        for i, (a, b) in enumerate(segs):
-            f = V(fb, a - first, b - first)
-            w = b - a
-            c = float(1 + W1 - 2 * W2 + (W1 if i < hm else 0))
-            act(V("fs%d" % t, CW * i, CW * i + w), f, Act.Sign, bias=V(jj, 6 + i, 7 + i), scale=-1.0, accum=V("sa%d" % t, i, i + 1))
-            if i < hm:
-                act(V("fs%d" % t, CW * (6 + i), CW * (6 + i) + w), f, Act.Sign, bias=V(jj, 12 + i, 13 + i), scale=-1.0, accum=V("sb%d" % t, i, i + 1))
-                ts(V("ch%d" % t, 2 * HW * i, 2 * HW * i + w), f, V(jj, 6 + i, 7 + i), c, Alu.is_le, Alu.mult)
+            jj, o = "jj%d" % t, 0
+            ts(V(jj), V("jt%d" % t, 6, 18), V(fb, PAD + n, PAD + n + 1), None, Alu.add)
+            if t == 0:
+                ts(V("xc%d" % t), V(jj, 6, 7), float(SW), None, Alu.mult)
             else:
-                o = CW * (i - hm)
-                ts(V("ca%d" % t, o, o + w), f, V(jj, 6 + i, 7 + i), c, Alu.is_le, Alu.mult)
-                ts(V("cp%d" % t, o, o + w), f, V(jj, 12 + i, 13 + i), float(-W1), Alu.is_le, Alu.mult)
-        scan(V("cuh%d" % t, 1, 1 + hm * HW), V("ch%d" % t, 0, 2 * hm * HW, 2), V("ch%d" % t, 1, 2 * hm * HW, 2), 0.0, Alu.add, Alu.add)
-        scan(V("cum%d" % t, 1, 1 + z * CW), V("ca%d" % t, 0, z * CW), V("cp%d" % t, 0, z * CW), 0.0, Alu.add, Alu.add)
+                act(V("xc%d" % t), V(jj, 6, 7), Act.Copy, scale=float(SW))
+        nv = min(m, NV[t])
+        hm = m - nv
+        for i in range(m):
+            x, y = slice_of(t, i)
+            ts(V("ch%d" % t, CW * i, CW * i + SW), V(fb, x, y), V(jj, o + i, o + i + 1), V(jj, o + 6 + i, o + 7 + i), Alu.max, Alu.min)
+            if i < hm:
+                act(V("fs%d" % t, CW * i, CW * i + CW), V("ch%d" % t, CW * i, CW * i + CW), Act.Copy, accum=V("sm%d" % t, i, i + 1))
+        cu, h = "cu%d" % t, CW // 2
+        scan(V(cu, 1, 1 + nv * h), V("ch%d" % t, hm * CW, m * CW, 2), V("ch%d" % t, hm * CW + 1, m * CW, 2), 0.0, Alu.add, Alu.add)
         fillin(jobs)
-        tt(V("dd%d" % t, 0, hm), V("cuh%d" % t, HW, hm * HW + 1, HW), V("cuh%d" % t, 0, (hm - 1) * HW + 1, HW), Alu.subtract)
-        ts(V("xa%d" % t, 0, m), V("sa%d" % t, 0, m), float(W2), None, Alu.mult)
-        ts(V("xb%d" % t, 0, hm), V("sb%d" % t, 0, hm), float(-W1), None, Alu.mult)
-        tt(V("dd%d" % t, hm, m), V("cum%d" % t, CW, z * CW + 1, CW), V("cum%d" % t, 0, (z - 1) * CW + 1, CW), Alu.subtract)
-        tt(V("xa%d" % t, 0, hm), V("xa%d" % t, 0, hm), V("xb%d" % t, 0, hm), Alu.add)
-        tt(V("ll%d" % t, 0, m), V("dd%d" % t, 0, m), V("xa%d" % t, 0, m), Alu.add)
+        sm, W = V("sm%d" % t, 0, m), NW[t]
+        tt(V("sm%d" % t, hm, m), V(cu, h, nv * h + 1, h), V(cu, 0, (nv - 1) * h + 1, h), Alu.subtract)
+        ts(V("qi%d" % t, 0, m), sm, V("xc%d" % t), -1.0 / 6, Alu.subtract, Alu.mult)
+        ts(V("ws%d" % t, 0, m), sm, V("xc%d" % t), -0.5 * W, Alu.subtract, Alu.mult)
+        ts(V("wy%d" % t, 0, m), V("qi%d" % t, 0, m), float(1 - 3 * W), float(W), Alu.mult, Alu.add)
+        tt(V("ll%d" % t, 0, m), V("ws%d" % t, 0, m), V("wy%d" % t, 0, m), Alu.add)
         for b in range(4):
             for a in range(4):
-                copy("vs"[(a + b) % 2], V("wf%d" % t, a, 4 * m, 4, 32 * b, 32 * b + 32), V("ll%d" % t, 0, m, 1, 32 * a, 32 * a + 32))
+                copy("s" if (a + b) % 2 and (a, b) != (0, 1) else "v", V("wf%d" % t, a, 4 * m, 4, 32 * b, 32 * b + 32), V("ll%d" % t, 0, m, 1, 32 * a, 32 * a + 32))
         while jobs:
             fillin(jobs)
         copy("v", V("wu%d" % t, 0, 4 * m), V("wf%d" % t, 0, 4 * m))
@@ -456,9 +460,9 @@ def rank_program(g, core, T, topo):
     def pick(t, x=0, y=None):
         y, w = y or NW[t + 1], 3 * NW[t]
         off = V("wu%d" % t, x // 16, y // 16)
-        a, b = V("r%dc" % t, 0, w), V("r%dc" % (t + 1), x, y)
+        a, b = V("r%dc" % t, 0, w), V("r%dc" % (t + 1), C[t + 1] + x, C[t + 1] + y)
         op("v", lambda: g.vector.tensor_copy(b[0].bitcast(dt.uint32), a[0].bitcast(dt.uint32).indirect(off[0])), [a, off], [b])
-        c, d = V("r%ds" % t, 0, w), V("r%ds" % (t + 1), x, y)
+        c, d = V("r%ds" % t, 0, w), V("r%ds" % (t + 1), C[t + 1] + x, C[t + 1] + y)
         op("s", lambda: g.scalar.activation(d[0], c[0].indirect(off[0]), Act.Copy), [c, off], [d])
 
     def numbers(t, out):
@@ -467,14 +471,24 @@ def rank_program(g, core, T, topo):
         op("s", lambda: g.scalar.activation(out[0], a[0].indirect(off[0]), Act.Copy), [a, off], [out])
 
     border = [(0, own0[0])] * (own0[0] > 0) + [(own0[1], NW[0])] * (own0[1] < NW[0])
+    if len(border) == 2:
+        jobs = [(0, 144, 288), None, None, None, None, (1, 0, NW[0]), (0, 0, 144), (0, 288, NW[0])]
+    elif r == 0:
+        jobs = [(0, 0, 144), None, None, None, None, (1, 0, NW[0]), (0, 144, NW[0])]
+    else:
+        jobs = [(0, 144, NW[0]), None, None, None, None, (1, 0, NW[0]), (0, 0, 144)]
+    inner = jobs.pop(0)
 
     def flight_of_scores0():
+        last_steps(0)
         quant("a", 0, 512, V("at"))
 
     def flight_of_counts0():
-        kids(0, "ssssssss", range(4), own0)
+        kids(0, "vsvsssss", range(4), own0)
         quant("b", 0, 512, V("bt"))
-        kids(0, "ssssssss", range(4, 5))
+        kidq(0, [inner])[0]()
+        kids(0, "ssssssss", range(4, 5), own0)
+        steps(1)
         for i in range(3):
             op("g", lambda: g.iota(T.tn0[:, NW[0] * i:NW[0] * i + NW[0]], [[4, NW[0]]], 4 * WIN[0][r][0] + (2 if i == 2 else 0), 0, allow_small_or_imprecise_dtypes=True),
                [], [V("tn0", NW[0] * i, NW[0] * i + NW[0])])
@@ -482,24 +496,21 @@ def rank_program(g, core, T, topo):
     def rest_kids():
         kids(0, "ssssssss", range(5, 8))
         for x in border:
+            kids(0, "ssssssss", range(4, 5), x)
+        for x in border:
             kids(0, "ssssssss", range(4), x)
-    if len(border) == 2:
-        jobs = [(0, 144, 288), None, None, None, (1, 0, NW[0]), (0, 0, 144), (0, 288, NW[0])]
-    elif r == 0:
-        jobs = [(0, 0, 144), None, None, None, (1, 0, NW[0]), (0, 144, NW[0])]
-    else:
-        jobs = [(0, 144, NW[0]), None, None, None, (1, 0, NW[0]), (0, 0, 144)]
-    order(0, 1, flight_of_scores0, flight_of_counts0, rest_kids, kidq(0, jobs))
+    order(0, flight_of_scores0, flight_of_counts0, rest_kids, kidq(0, jobs))
     pick(0)
     score(1)
     bank[0] = 0
 
     def flight_of_scores1():
+        last_steps(1)
         kids(1, "sss", range(3))
+        quant("w", 0, 128, V("wt"))
 
     def flight_of_counts1():
-        kids(1, "sssvvvss", range(3, 8))
-        quant("w", 0, 128, V("wt"))
+        kids(1, "ssssvsvs", range(3, 8))
         for job in kidq(1, [(0, 0, NW[1]), (1, 0, NW[1])]):
             job()
 
@@ -507,21 +518,17 @@ def rank_program(g, core, T, topo):
         numbers(0, V("tn1", 0, NW[1]))
         copy("s", V("tn1", NW[1], 2 * NW[1]), V("tn1", 0, NW[1]))
         act(V("tn1", 2 * NW[1], 3 * NW[1]), V("tn1", 0, NW[1]), Act.Identity, bias=1.0)
-    order(1, 1, flight_of_scores1, flight_of_counts1, new_numbers, [])
+    order(1, flight_of_scores1, flight_of_counts1, new_numbers, [])
     cut = ((0, 160), (160, E))
     for x, y in cut:
         pick(1, x, y)
     outs = [mm(("psc", i), "w", 0, "r2", x, y - x) for i, (x, y) in enumerate(cut)]
     numbers(1, V("hsr"))
 
-    def scales(q, k):
-        dma(q, T.osc[4 * k:4 * k + 4, :], T.r2s[32 * k:32 * k + 4, :], "out", [V("r2s")], [])
     for x, y in cut:
         dma("y", T.oc[:, 4 * x:4 * y], codes("r2c", x, y), "out", [V("r2c", x, y)], [])
-    scales("y", 0)
-    scales("y", 1)
-    scales("s", 2)
-    scales("s", 3)
+    for k in range(4):
+        dma("y", T.osc[4 * k:4 * k + 4, :], T.r2s[32 * k:32 * k + 4, :], "out", [V("r2s")], [])
     dma("s", T.hs[:], T.hsr[0:1, :], "out", [V("hsr")], [])
     for o, (x, y) in zip(outs, cut):
         copy("v", V("ysb", x, y), o)

from concourse.bass import DstId, RemoteDMATransfer
from concourse.mybir import dt, AluOpType as Alu, AxisListType, ActivationFunctionType as Act

N, P, K, E = 4, 256, 64, 288
LEN = (1024, 1088)
CH = ([(128 * c, 0, 4, c // 2) for c in range(8)],
      [(0, 0, 4, 0), (128, 0, 4, 0), (256, 0, 4, 1), (384, 0, 4, 1), (512, 0, 4, 2), (640, 0, 4, 2), (736, 1, 3, 2), (832, 0, 4, 3), (960, 0, 4, 3)])
WIN = ([(0, 288), (160, 576), (448, 864), (736, 1024)], [(0, 288), (224, 576), (512, 864), (800, 1088)], [(E * r, E * r + E) for r in range(N)])
NEED = ([(0, 288), (0, 576), (448, 1024), (736, 1024)], [(0, 288), (0, 576), (512, 1088), (800, 1088)])
F32, BF, I32, U16 = "float32", "bfloat16", "int32", "uint16"
SW = 130
CW = 132
PAD = 64
NV = (6, 3)
CMPW = 448

SCRATCH = {
    "xt": ("sbuf", [128, 1024], BF), "uin": ("sbuf", [128, 8], BF), "ut": ("sbuf", [128, 512], BF), "uz": ("sbuf", [128, 128], BF),
    "at": ("sbuf", [128, 2048], BF), "bt": ("sbuf", [128, 2048], BF), "wt": ("sbuf", [128, 512], BF),
    "msp": ("sbuf", [128, 640], BF), "mrep": ("sbuf", [128, 640], BF), "carb": ("sbuf", [128, 640], BF),
    "pi": ("sbuf", [128, 4], I32), "dcol": ("sbuf", [128, 2], F32),
    "psc": ("psum", [128, 2048], F32), "pch": ("psum", [128, 2048], F32),
    "ysb": ("sbuf", [128, 288], F32), "hsr": ("sbuf", [128, 288], F32),
    "tn0": ("sbuf", [128, 1248], F32), "tn1": ("sbuf", [128, 1056], F32),
}
for _q, _n in (("u", 128), ("a", 512), ("b", 512), ("w", 128), ("r0", 1248), ("r1", 1056), ("r2", 288)):
    SCRATCH[_q + "c"] = ("sbuf", [128, _n], "float8_e4m3fn_x4")
    SCRATCH[_q + "s"] = ("sbuf", [128, _n], "uint8")
for _t in range(2):
    for _n, _w, _d in (("ha", 1664, BF), ("hb", 1664, BF), ("own", 4, F32), ("land", 8, F32), ("cmp", 9 * CMPW, BF),
                       ("eq", 384, BF), ("sg", 3 * 320, BF), ("sj", 3 * 320, BF), ("so", 9 * CMPW // 2, BF), ("acc", 3, F32),
                       ("pland", 16, BF), ("rho", 15, F32), ("mrow", 640, BF), ("inc", 704, BF), ("fb", 752, BF),
                       ("jt", 18, F32), ("jj", 12, F32), ("xc", 1, F32), ("ch", 6 * CW, BF), ("fs", 6 * CW, BF), ("cu", 1 + 6 * CW // 2, F32),
                       ("sm", 6, F32), ("qi", 6, I32), ("ws", 6, F32), ("wy", 6, F32), ("ll", 6, F32), ("wf", 24, F32), ("wu", 24, U16)):
        SCRATCH["%s%d" % (_n, _t)] = ("sbuf", [128, _w], _d)
SEMAPHORES = ["v", "s", "p", "gc", "sent", "arrw", "dx0", "dx1", "du", "da", "db", "dw", "out"] + ["%s%d_%d" % (k, t, r) for k in ("arr", "cnt") for t in range(2) for r in range(N)]


def rank_program(g, core, T, topo):
    r = T.rank_of(core)
    if r is None:
        return
    Q = {"v": g.vector, "s": g.scalar, "p": g.tensor, "g": g, "y": g.sync}
    ESEM = {"v": "v", "s": "s", "p": "p", "g": "gc"}
    total, known, hist = {}, {q: {} for q in Q}, {}

    def V(name, c0=0, c1=None, step=1, p0=0, p1=128):
        if c1 is None:
            c1 = SCRATCH[name][1][1]
        ap = T[name][p0:p1, c0:c1] if step == 1 else T[name][p0:p1, c0:c1:step]
        return (ap, name, c0, c1, step, p0, p1)

    def clash(x, y):
        if SCRATCH[x[1]][0] == "psum":
            return x[2] // 512 <= (y[3] - 1) // 512 and y[2] // 512 <= (x[3] - 1) // 512
        if x[6] <= y[5] or y[6] <= x[5] or x[3] <= y[2] or y[3] <= x[2]:
            return False
        return not (x[4] == y[4] and x[4] > 1 and (x[2] - y[2]) % x[4] != 0)

    def need(q, reads, writes):
        todo = {}
        for acc, wr in [(a, False) for a in reads] + [(a, True) for a in writes]:
            psum = SCRATCH[acc[1]][0] == "psum"
            for old, owr, s, n, clock, oq in hist.get(acc[1], []):
                if not (wr or owr or (psum and oq != q)) or known[q].get(s, 0) >= n or not clash(acc, old):
                    continue
                if s not in todo or todo[s][0] < n:
                    todo[s] = (n, clock)
        for s in sorted(todo):
            n, clock = todo[s]
            if known[q].get(s, 0) < n:
                Q[q].wait_ge(T.sem[s], n)
                known[q][s] = n
                for s2, n2 in clock.items():
                    known[q][s2] = max(known[q].get(s2, 0), n2)

    def note(q, reads, writes, s, n):
        clock = dict(known[q])
        for acc, wr in [(a, False) for a in reads] + [(a, True) for a in writes]:
            hist.setdefault(acc[1], []).append((acc, wr, s, n, clock, q))

    def op(q, call, reads, writes):
        need(q, reads, writes)
        s = ESEM[q]
        total[s] = total.get(s, 0) + 1
        call().then_inc(T.sem[s], 1)
        note(q, reads, writes, s, total[s])

    def dma(q, out, in_, sem, reads, writes):
        need(q, reads, writes)
        total[sem] = total.get(sem, 0) + 16
        Q[q].dma_start(out, in_).then_inc(T.sem[sem], 16)
        note(q, reads, writes, sem, total[sem])

    def sc(x):
        return x[0] if isinstance(x, tuple) else x

    def ts(out, in0, s1, s2, op0, op1=None):
        rd = [x for x in (in0, s1, s2) if isinstance(x, tuple)]
        if op1 is None:
            op("v", lambda: g.vector.tensor_scalar(out[0], in0[0], sc(s1), None, op0), rd, [out])
        else:
            op("v", lambda: g.vector.tensor_scalar(out[0], in0[0], sc(s1), sc(s2), op0, op1), rd, [out])

    def tt(out, a, b, o):
        op("v", lambda: g.vector.tensor_tensor(out[0], a[0], b[0], o), [a, b], [out])

    def copy(q, out, in_):
        if q == "v":
            op("v", lambda: g.vector.tensor_copy(out[0], in_[0]), [in_], [out])
        else:
            op("s", lambda: g.scalar.activation(out[0], in_[0], Act.Copy), [in_], [out])

    def act(out, in_, f, bias=0.0, scale=1.0, accum=None):
        rd = [in_] + [x for x in (bias, scale) if isinstance(x, tuple)]
        if accum is None:
            op("s", lambda: g.scalar.activation(out[0], in_[0], f, bias=sc(bias), scale=sc(scale)), rd, [out])
        else:
            op("s", lambda: g.scalar.activation(out[0], in_[0], f, bias=sc(bias), scale=sc(scale), accum_out=accum[0]), rd, [out, accum])

    def scan(out, a, b, initial, o0, o1):
        op("v", lambda: g.vector.tensor_tensor_scan(out[0], a[0], b[0], initial, o0, o1), [a, b], [out])

    def turn(out, in_):
        op("v", lambda: g.vector.transpose(out[0], in_[0]), [in_], [out])

    def fill(out, c):
        op("v", lambda: g.vector.memset(out[0], c), [], [out])

    def quant(q, a, b, in_):
        c, s = V(q + "c", a, b), V(q + "s", a, b)
        op("v", lambda: g.vector.quantize_mx(c[0], s[0], in_[0]), [in_], [c, s])

    def mm(bank, q1, a1, q2, a2, n):
        o = V(bank[0], 512 * bank[1], 512 * bank[1] + n)
        w, ws, x, xs = V(q1 + "c", a1, a1 + 128), V(q1 + "s", a1, a1 + 128), V(q2 + "c", a2, a2 + n), V(q2 + "s", a2, a2 + n)
        op("p", lambda: g.tensor.matmul_mx(o[0], w[0], ws[0], x[0], xs[0], True, True), [w, ws, x, xs], [o])
        return o

    def dst(c):
        rid, pid = topo.addr(c)[:2]
        return DstId(rid=rid, pnc=pid)

    def engines(cs):
        return sorted(set.intersection(*[set(topo.engines(core, c)) for c in cs]))

    def send(outs, src, cs, sem):
        e = engines(cs)
        need("g", [src], [])
        g.remote_dma_fused([RemoteDMATransfer(dst_ids=[dst(c) for c in cs], dma_engine_mask=sum(1 << k for k in e), remote_sem=T.sem[sem],
                                              srcs=[src[0]], dsts=outs)], local_sem=T.sem.sent)
        total["sent"] = total.get("sent", 0) + len(e)

    def arrive(sem, n, views):
        total[sem] = total.get(sem, 0) + n
        for v in views:
            hist.setdefault(v[1], []).append((v, True, sem, total[sem], {}, None))

    def codes(name, a, b):
        return T[name][:, a:b].bitcast(dt.uint8)

    def near(c, d):
        return topo.same_plane(topo.chip(c), topo.chip(d))

    def targets(c):
        i = T.rank_of(c)
        return sorted([d for d in T.cores if d != c], key=lambda d: (near(c, d), (T.rank_of(d) - i) % N))

    NW = [WIN[t][r][1] - WIN[t][r][0] for t in range(3)]
    C = (NW[0], NW[1], 0)
    others = targets(core)
    others_r = [T.rank_of(c) for c in others]
    ENG = len(engines(others))
    half = (T.cores[:N // 2], T.cores[N // 2:])

    def slot(me, s):
        return s if s < me else s - 1

    def group(me, t):
        return list(range(5)) if me < N // 2 else list(range(len(CH[t]) - 5, len(CH[t])))

    def landpos(me, t):
        return {k: i for i, k in enumerate([k for k, c in enumerate(CH[t]) if c[3] != me])}

    for i in range(2):
        dma("y", T.xt[:, 512 * i:512 * i + 512], T.x[:, 512 * i:512 * i + 512], "dx%d" % i, [], [V("xt", 512 * i, 512 * i + 512)])
    dma("s", T.uin[:, 0:4], T.u[:, 0:4], "du", [], [V("uin", 0, 4)])
    dma("y", T.at[:], T.a[:], "da", [], [V("at")])
    dma("y", T.bt[:], T.b[:], "db", [], [V("bt")])
    dma("y", T.wt[:], T.w[:], "dw", [], [V("wt")])

    own0 = (P * r - WIN[0][r][0], P * r - WIN[0][r][0] + P)
    nb = [s for s in (r - 1, r + 1) if 0 <= s < N]
    wviews = []
    for s in nb:
        a, b = (0, own0[0]) if s < r else (own0[1], NW[0])
        wviews += [V("r0c", C[0] + a, C[0] + b), V("r0s", C[0] + a, C[0] + b)]
    arrive("arrw", 2 * ENG * len(nb), wviews)
    for t in range(2):
        for s in others_r:
            cols = [landpos(r, t)[k] for k, c in enumerate(CH[t]) if c[3] == s]
            arrive("arr%d_%d" % (t, s), ENG, [V("land%d" % t, cols[0], cols[-1] + 1)])
            arrive("cnt%d_%d" % (t, s), ENG, [V("pland%d" % t, 5 * slot(r, s), 5 * slot(r, s) + 5)])

    plan = []
    for t in range(2):
        a, b = NEED[t][r]
        chunks = [k for k, c in enumerate(CH[t]) if c[0] + 32 * c[2] > a and c[0] + 32 * c[1] < b]
        back = a > 0
        end = WIN[t][r][1]
        lo1, hi1 = WIN[t + 1][r]
        mid = (lo1 + end) // 2 if back else (lo1 + hi1) // 2
        plan.append((chunks, a, b - a, back, end, mid, (hi1 - lo1 + 63) // 64))

    def runs(chs, base, size):
        out = []
        for i, c in enumerate(chs):
            lo, hi = max(c[0] + 32 * c[1], base), min(c[0] + 32 * c[2], base + size)
            x, y, w = 128 * i + lo - c[0], lo - base, hi - lo
            if out and out[-1][0] + out[-1][2] == x and out[-1][1] + out[-1][2] == y:
                out[-1] = (out[-1][0], out[-1][1], out[-1][2] + w)
            else:
                out.append((x, y, w))
        return out

    def slice_of(t, i):
        c = WIN[t + 1][r][0] + 64 * i - 64 - plan[t][1] + PAD
        return c, c + SW

    fill(V("uz"), 0.0)
    op("g", lambda: g.iota(T.pi[:, 0:1], [[0, 1]], 0, 1), [], [V("pi", 0, 1)])
    for t in range(2):
        e = -1 - K - plan[t][4] if plan[t][3] else -1 - plan[t][5]
        op("g", lambda: g.iota(T["jt%d" % t][:, 0:6], [[64, 6]], WIN[t + 1][r][0] + e, 1, allow_small_or_imprecise_dtypes=True), [], [V("jt%d" % t, 0, 6)])
    op("v", lambda: g.vector.tensor_scalar(T.pi[:, 1:2], T.pi[:, 0:1], 96, None, Alu.bitwise_and), [V("pi", 0, 1)], [V("pi", 1, 2)])
    op("v", lambda: g.vector.tensor_scalar(T.pi[:, 2:3], T.pi[:, 0:1], 16, None, Alu.bitwise_and), [V("pi", 0, 1)], [V("pi", 2, 3)])
    ts(V("dcol", 0, 1), V("pi", 1, 2), -1.0, None, Alu.mult)
    ts(V("dcol", 1, 2), V("pi", 2, 3), -2.0, V("dcol", 0, 1), Alu.mult, Alu.add)
    fill(V("msp"), 0.0)
    fill(V("carb"), 1.0)
    fill(V("carb", 0, 640, 32), 0.0)

    def steps(t):
        chunks, first, n, back, end, mid, m = plan[t]
        for x, y, w in runs([CH[t][k] for k in chunks], first, n):
            odd = x // 32 % 2
            n2 = (w + 63) // 64
            op("g", lambda: g.iota(T["inc%d" % t][:, y:y + 64 * n2], [[0, n2], [1 - 2 * odd, 2], [0, 32]], 2 + odd, 0, allow_small_or_imprecise_dtypes=True),
               [], [V("inc%d" % t, y, y + 64 * n2)])

    def last_steps(t):
        chunks, first, n, back, end, mid, m = plan[t]
        x, y, w = runs([CH[t][k] for k in chunks], first, n)[-1]
        last = 2 + (x + w - 32) // 32 % 2
        far = 2 * (first + n - end)
        if far:
            fill(V("inc%d" % t, n - 1, n), float(last - 256))
            fill(V("inc%d" % t, n - 2, n - 1), float(last - (far - 256)))

    def tables(t):
        chunks, first, n, back, end, mid, m = plan[t]
        fb, lo1 = "fb%d" % t, WIN[t + 1][r][0]

        def put(out, c):
            act(out, V("uz", 0, out[3] - out[2]), Act.Identity, bias=float(c))
        put(V(fb, PAD, PAD + 1), 2 * (first - mid))
        if slice_of(t, 0)[0] < PAD:
            put(V(fb, 0, PAD), -600)
        z = slice_of(t, m - 1)[1]
        if z > PAD + n + 1:
            put(V(fb, PAD + n + 1, z), 600)
        put(V("cu%d" % t, 0, 1), 0)
        for i in range(m):
            k = -(i * (128 * SW + 384) + 6 * (lo1 - 64 - WIN[t][r][0]) - 6)
            hi = (k // 512) * 512
            put(V("ch%d" % t, CW * i + SW, CW * i + SW + 1), hi)
            put(V("ch%d" % t, CW * i + SW + 1, CW * i + CW), k - hi)
        act(V("jt%d" % t, 6, 12), V("jt%d" % t, 0, 6), Act.Identity, bias=V("dcol", 1, 2), scale=2.0)
        act(V("jt%d" % t, 12, 18), V("jt%d" % t, 6, 12), Act.Identity, bias=6.0)
        if not back:
            act(V("xc%d" % t), V("jt%d" % t, 12, 13), Act.Copy, scale=float(SW))

    steps(0)
    tables(0)
    tables(1)
    for k in range(4):
        ts(V("ut", k, 512, 4), V("uz"), V("uin", k, k + 1), None, Alu.add)
    quant("u", 0, 128, V("ut"))
    for i in range(2):
        quant("r0", C[0] + own0[0] + 128 * i, C[0] + own0[0] + 128 * i + 128, V("xt", 512 * i, 512 * i + 512))

    def score(t):
        q = "r%d" % t
        w0 = WIN[t][r][0] - C[t]
        mine = [c for c in CH[t] if c[3] == r]
        n = len(mine)
        for i, c in enumerate(mine):
            mm(("psc", 1 + i), q, c[0] - w0, "u", 0, 128)
        lo, hi = mine[0][0] + 32 * mine[0][1], mine[-1][0] + 32 * mine[-1][2]
        mm(("psc", 0), "u", 0, q, lo - w0, hi - lo)
        mm(("pch", 3), "u", 0, q, lo - w0, hi - lo)
        ow = V("own%d" % t, 0, n)
        copy("v", ow, V("psc", 512, 512 * n + 1, 512))
        outs = []
        for c in others:
            p = landpos(T.rank_of(c), t)[CH[t].index(mine[0])]
            outs.append(T["land%d" % t][:, p:p + n])
        send(outs, ow, others, "arr%d_%d" % (t, r))

    score(0)
    for s in nb:
        sw = WIN[0][s]
        lo, hi = max(P * r, sw[0]), min(P * r + P, sw[1])
        a, b = lo - WIN[0][r][0] + C[0], hi - WIN[0][r][0] + C[0]
        e = sw[1] - sw[0] - sw[0]
        c, d = lo + e, hi + e
        send([codes("r0c", c, d)], (codes("r0c", a, b),) + V("r0c", a, b)[1:], [T.cores[s]], "arrw")
        send([T.r0s[:, c:d]], V("r0s", a, b), [T.cores[s]], "arrw")
    bank = [0]

    def kids(t, qs, part, cols=None):
        q, w = "r%d" % t, NW[t]
        lo, hi = cols or (0, w)
        m0 = max(0, min(lo, hi - 128))
        n = max(hi, m0 + 128) - m0
        for i in part:
            buf, k = (("pch", 0), ("pch", 1), ("pch", 2), ("psc", 1), ("psc", 2), ("psc", 3))[bank[0] % 6]
            bank[0] += 1
            mm((buf, k), "ab"[i // 4], 128 * (i % 4), q, C[t] + m0, n)
            o = V(buf, 512 * k + lo - m0, 512 * k + hi - m0)
            h = V("h%s%d" % ("ab"[i // 4], t), 4 * lo + i % 4, 4 * hi, 4)
            if qs[i] == "v":
                ts(h, o, 0.0625, None, Alu.mult)
            else:
                act(h, o, Act.Copy, scale=0.0625)

    def kidq(t, pieces):
        q, w = "r%d" % t, NW[t]
        return [p and (lambda k=p[0], x=p[1], y=p[2]: quant(q, 2 * k * w + x, 2 * k * w + y, V("h%s%d" % ("ab"[k], t), 4 * x, 4 * y))) for p in pieces]

    def fillin(jobs):
        job = jobs.pop(0) if jobs else None
        if job:
            job()

    def order(t, flight1, flight2, hook2, jobs):
        chunks, first, n, back, end, mid, m = plan[t]
        lp = landpos(r, t)
        land, so, z = "land%d" % t, "so%d" % t, CMPW // 2
        chunks_of = [[k for k, c in enumerate(CH[t]) if c[3] == s] for s in range(N)]
        mine = chunks_of[r]
        lo = CH[t][mine[0]][0] + 32 * CH[t][mine[0]][1]
        hi = CH[t][mine[-1]][0] + 32 * CH[t][mine[-1]][2]
        W = hi - lo

        def row(a, b):
            return V("psc", a - lo, b - lo)

        def total_of(k, w):
            x, y = CMPW * k, w // 2
            scan(V(so, 9 * (z - y) + k, 9 * (z - 1) + k + 1, 9), V("cmp%d" % t, x, x + y), V("cmp%d" % t, x + y, x + w), 0.0, Alu.add, Alu.add)

        def part(k, m=1):
            return V(so, 9 * (z - 1) + k, 9 * (z - 1) + k + m, 9 if m == 1 else 1)

        wide = {}
        for i, k in enumerate(mine):
            s = CH[t][k][0]
            e = min(s + 128, hi)
            val = V("own%d" % t, i, i + 1)
            x = CMPW * k
            q = V("eq%d" % t, 128 * i, 128 * i + e - s)
            d = V("cmp%d" % t, x + W, x + W + e - s)
            ts(q, row(s, e), val, None, Alu.is_equal)
            op("g", lambda: g.affine_select(d[0], q[0], [[-1, e - s]], Alu.is_gt, 0.0, 0, 1), [q], [d])
            if s > lo:
                ts(V("cmp%d" % t, x, x + s - lo), row(lo, s), val, None, Alu.is_ge)
            ts(V("cmp%d" % t, x + s - lo, x + W), row(s, hi), val, None, Alu.is_gt)
            wide[k] = W + e - s
        flight1()
        first_r, second_r, third_r = sorted(others_r, key=lambda s: targets(T.cores[s]).index(core))
        byS, byV = (third_r, second_r) if len(chunks_of[second_r]) > len(chunks_of[third_r]) else (second_r, third_r)
        for i, k in enumerate(chunks_of[byS]):
            act(V("sg%d" % t, 320 * i, 320 * i + W), V("pch", 1536, 1536 + W), Act.Sign, bias=V(land, lp[k], lp[k] + 1), scale=-1.0)
            act(V("sj%d" % t, 320 * i, 320 * i + W), V("sg%d" % t, 320 * i, 320 * i + W), Act.Relu, scale=1.0 if r < byS else -1.0, accum=V("acc%d" % t, i, i + 1))
            act(part(k), V("acc%d" % t, i, i + 1), Act.Copy, scale=-1.0 if r < byS else 1.0, bias=float(W) if r < byS else 0.0)
        last = None
        for s in (first_r, byV):
            for k in chunks_of[s]:
                ts(V("cmp%d" % t, CMPW * k, CMPW * k + W), row(lo, hi), V(land, lp[k], lp[k] + 1), None, Alu.is_ge if r < s else Alu.is_gt)
                if last is not None:
                    total_of(last, W)
                last = k
        total_of(last, W)
        for k in mine:
            total_of(k, wide[k])
        for h in sorted(half, key=lambda h: core not in h):
            cs = [c for c in others if c in h]
            k0 = group(T.rank_of(h[0]), t)[0]
            send([T["pland%d" % t][:, 5 * slot(T.rank_of(c), r):5 * slot(T.rank_of(c), r) + 5] for c in cs], part(k0, 5), cs, "cnt%d_%d" % (t, r))
        flight2()
        k0, nc = chunks[0], len(chunks)
        o = chunks[0] - group(r, t)[0]
        at = part(k0, nc)
        for i, s in enumerate(sorted(others_r, key=lambda s: (s // 2 != r // 2, near(core, T.cores[s])))):
            to = V("rho%d" % t, 5 * i, 5 * i + nc)
            tt(to, at, V("pland%d" % t, 5 * slot(r, s) + o, 5 * slot(r, s) + o + nc), Alu.add)
            at = to
        for b in range(4):
            for a in range(4):
                src = V("rho%d" % t, 10, 10 + nc, 1, 32 * a, 32 * a + 32)
                to = V("msp", 32 * a, 128 * nc, 128, 32 * b, 32 * b + 32)
                if a % 2:
                    act(to, src, Act.Sign, bias=K - 0.5, scale=-1.0)
                else:
                    ts(to, src, float(K), 2.0, Alu.is_lt, Alu.mult)
        hook2()
        fillin(jobs)
        pieces = runs([CH[t][k] for k in chunks], first, n)
        x0, x1 = pieces[0][0], pieces[-1][0] + pieces[-1][2]
        scan(V("mrep", x0, x1), V("carb", x0, x1), V("msp", x0, x1), 0.0, Alu.mult, Alu.add)
        fillin(jobs)
        for x, y, w in pieces:
            turn(V("mrow%d" % t, y, y + w), V("mrep", x, x + w))
        fillin(jobs)
        fb = "fb%d" % t
        scan(V(fb, PAD + 1, PAD + n + 1), V("mrow%d" % t, 0, n), V("inc%d" % t, 0, n), float(2 * (first - mid)), Alu.add, Alu.add)
        fillin(jobs)
        jj, o = "jt%d" % t, 6
        if back:
            jj, o = "jj%d" % t, 0
            ts(V(jj), V("jt%d" % t, 6, 18), V(fb, PAD + n, PAD + n + 1), None, Alu.add)
            if t == 0:
                ts(V("xc%d" % t), V(jj, 6, 7), float(SW), None, Alu.mult)
            else:
                act(V("xc%d" % t), V(jj, 6, 7), Act.Copy, scale=float(SW))
        nv = min(m, NV[t])
        hm = m - nv
        for i in range(m):
            x, y = slice_of(t, i)
            ts(V("ch%d" % t, CW * i, CW * i + SW), V(fb, x, y), V(jj, o + i, o + i + 1), V(jj, o + 6 + i, o + 7 + i), Alu.max, Alu.min)
            if i < hm:
                act(V("fs%d" % t, CW * i, CW * i + CW), V("ch%d" % t, CW * i, CW * i + CW), Act.Copy, accum=V("sm%d" % t, i, i + 1))
        cu, h = "cu%d" % t, CW // 2
        scan(V(cu, 1, 1 + nv * h), V("ch%d" % t, hm * CW, m * CW, 2), V("ch%d" % t, hm * CW + 1, m * CW, 2), 0.0, Alu.add, Alu.add)
        fillin(jobs)
        sm, W = V("sm%d" % t, 0, m), NW[t]
        tt(V("sm%d" % t, hm, m), V(cu, h, nv * h + 1, h), V(cu, 0, (nv - 1) * h + 1, h), Alu.subtract)
        ts(V("qi%d" % t, 0, m), sm, V("xc%d" % t), -1.0 / 6, Alu.subtract, Alu.mult)
        ts(V("ws%d" % t, 0, m), sm, V("xc%d" % t), -0.5 * W, Alu.subtract, Alu.mult)
        ts(V("wy%d" % t, 0, m), V("qi%d" % t, 0, m), float(1 - 3 * W), float(W), Alu.mult, Alu.add)
        tt(V("ll%d" % t, 0, m), V("ws%d" % t, 0, m), V("wy%d" % t, 0, m), Alu.add)
        for b in range(4):
            for a in range(4):
                copy("s" if (a + b) % 2 and (a, b) != (0, 1) else "v", V("wf%d" % t, a, 4 * m, 4, 32 * b, 32 * b + 32), V("ll%d" % t, 0, m, 1, 32 * a, 32 * a + 32))
        while jobs:
            fillin(jobs)
        copy("v", V("wu%d" % t, 0, 4 * m), V("wf%d" % t, 0, 4 * m))

    def pick(t, x=0, y=None):
        y, w = y or NW[t + 1], 3 * NW[t]
        off = V("wu%d" % t, x // 16, y // 16)
        a, b = V("r%dc" % t, 0, w), V("r%dc" % (t + 1), C[t + 1] + x, C[t + 1] + y)
        op("v", lambda: g.vector.tensor_copy(b[0].bitcast(dt.uint32), a[0].bitcast(dt.uint32).indirect(off[0])), [a, off], [b])
        c, d = V("r%ds" % t, 0, w), V("r%ds" % (t + 1), C[t + 1] + x, C[t + 1] + y)
        op("s", lambda: g.scalar.activation(d[0], c[0].indirect(off[0]), Act.Copy), [c, off], [d])

    def numbers(t, out):
        n, w = NW[t + 1], 3 * NW[t]
        off, a = V("wu%d" % t, 0, n // 16), V("tn%d" % t, 0, w)
        op("s", lambda: g.scalar.activation(out[0], a[0].indirect(off[0]), Act.Copy), [a, off], [out])

    border = [(0, own0[0])] * (own0[0] > 0) + [(own0[1], NW[0])] * (own0[1] < NW[0])
    if len(border) == 2:
        jobs = [(0, 144, 288), None, None, None, None, (1, 0, NW[0]), (0, 0, 144), (0, 288, NW[0])]
    elif r == 0:
        jobs = [(0, 0, 144), None, None, None, None, (1, 0, NW[0]), (0, 144, NW[0])]
    else:
        jobs = [(0, 144, NW[0]), None, None, None, None, (1, 0, NW[0]), (0, 0, 144)]
    inner = jobs.pop(0)

    def flight_of_scores0():
        last_steps(0)
        quant("a", 0, 512, V("at"))

    def flight_of_counts0():
        kids(0, "vsvsssss", range(4), own0)
        quant("b", 0, 512, V("bt"))
        kidq(0, [inner])[0]()
        kids(0, "ssssssss", range(4, 5), own0)
        steps(1)
        for i in range(3):
            op("g", lambda: g.iota(T.tn0[:, NW[0] * i:NW[0] * i + NW[0]], [[4, NW[0]]], 4 * WIN[0][r][0] + (2 if i == 2 else 0), 0, allow_small_or_imprecise_dtypes=True),
               [], [V("tn0", NW[0] * i, NW[0] * i + NW[0])])

    def rest_kids():
        kids(0, "ssssssss", range(5, 8))
        for x in border:
            kids(0, "ssssssss", range(4, 5), x)
        for x in border:
            kids(0, "ssssssss", range(4), x)
    order(0, flight_of_scores0, flight_of_counts0, rest_kids, kidq(0, jobs))
    pick(0)
    score(1)
    bank[0] = 0

    def flight_of_scores1():
        last_steps(1)
        kids(1, "sss", range(3))
        quant("w", 0, 128, V("wt"))

    def flight_of_counts1():
        kids(1, "ssssvsvs", range(3, 8))
        for job in kidq(1, [(0, 0, NW[1]), (1, 0, NW[1])]):
            job()

    def new_numbers():
        numbers(0, V("tn1", 0, NW[1]))
        copy("s", V("tn1", NW[1], 2 * NW[1]), V("tn1", 0, NW[1]))
        act(V("tn1", 2 * NW[1], 3 * NW[1]), V("tn1", 0, NW[1]), Act.Identity, bias=1.0)
    order(1, flight_of_scores1, flight_of_counts1, new_numbers, [])
    cut = ((0, 160), (160, E))
    for x, y in cut:
        pick(1, x, y)
    outs = [mm(("psc", i), "w", 0, "r2", x, y - x) for i, (x, y) in enumerate(cut)]
    numbers(1, V("hsr"))

    for x, y in cut:
        dma("y", T.oc[:, 4 * x:4 * y], codes("r2c", x, y), "out", [V("r2c", x, y)], [])
    for k in range(4):
        dma("y", T.osc[4 * k:4 * k + 4, :], T.r2s[32 * k:32 * k + 4, :], "out", [V("r2s")], [])
    dma("s", T.hs[:], T.hsr[0:1, :], "out", [V("hsr")], [])
    for o, (x, y) in zip(outs, cut):
        copy("v", V("ysb", x, y), o)
        dma("y", T.y[:, x:y], T.ysb[:, x:y], "out", [V("ysb", x, y)], [])
    for s in sorted(total):
        if known["g"].get(s, 0) < total[s]:
            g.wait_ge(T.sem[s], total[s])
